import numpy as np
import ml_dtypes


def mxq(x, axis, fmt="e4m3"):
    dtype, down = {"e4m3": (ml_dtypes.float8_e4m3fn, 7), "e5m2": (ml_dtypes.float8_e5m2, 14)}[fmt]
    v = np.moveaxis(np.asarray(x, np.float32).astype(ml_dtypes.bfloat16).astype(np.float64), axis, -1)
    blocks = v.reshape(v.shape[:-1] + (-1, 32))
    amax = np.abs(blocks).max(-1, keepdims=True)
    byte = np.maximum(np.where(amax > 0, np.frexp(amax)[1] - 1 + 127, 0) - down, 1)
    scale = np.exp2(byte - 127.0)
    codes = (blocks / scale).astype(np.float32).astype(dtype).astype(np.float64)
    return np.moveaxis((codes * scale).reshape(v.shape), -1, axis)


WIDE = False


def mx_kscale(k):
    if not WIDE:
        return np.ones(k)
    levels = np.array([30, -30])
    if k % 512:
        return np.exp2(np.random.permutation(np.resize(levels, k // 32))).repeat(32)
    a = np.empty((k // 512, 16))
    for p in range(k // 512):
        a[p, :8] = np.random.permutation(np.resize(levels, 8))
        for g in range(8):
            far = levels[np.abs(levels - a[p, g]) >= 10]
            a[p, g + 8] = far[np.random.randint(len(far))]
    return np.exp2(a.ravel()).repeat(32)


BF16 = ml_dtypes.bfloat16


def bf(x):
    return np.asarray(x, np.float32).astype(BF16)


def f64(x):
    return np.asarray(x).astype(np.float64)


B, L, P, H, D = 8, 256, 512, 1024, 512


def sigmoid(v):
    return 1.0 / (1.0 + np.exp(-v))


def setup_inputs():
    s, t, u = mx_kscale(P), mx_kscale(H), mx_kscale(H)
    c = np.random.standard_normal(H)
    head = np.random.standard_normal((P, H)) + 0.5 * np.random.standard_normal((P, 1)) + 0.5 * np.random.standard_normal((P, 1)) * c
    return {"d_logits": bf(np.random.standard_normal((B * L, P)) * s),
            "head_w": bf(head / np.sqrt(P) / s[:, None]),
            "spk_gain": bf(1 + 0.1 * np.random.standard_normal((B, H))),
            "normed": bf((np.random.standard_normal((B * L, H)) + 0.7 * c) / 1.22),
            "inv_std": bf(np.exp(0.3 * np.random.standard_normal(B * L))),
            "pre_a": bf(np.random.standard_normal((B * L, H))),
            "pre_b": bf(np.random.standard_normal((B * L, H))),
            "gain_a": bf((1 + 0.1 * np.random.standard_normal(H)) * t),
            "gain_b": bf((1 + 0.1 * np.random.standard_normal(H)) * u),
            "dir_a": bf(np.random.standard_normal((H, D)) / np.sqrt(H) / t[:, None]),
            "dir_b": bf(np.random.standard_normal((H, D)) / np.sqrt(H) / u[:, None])}


def reference(d_logits, head_w, spk_gain, normed, inv_std, pre_a, pre_b, gain_a, gain_b, dir_a, dir_b):
    dh = mxq(f64(d_logits), 1, "e4m3") @ mxq(f64(head_w), 0, "e4m3")
    dn = (dh.reshape(B, L, H) * f64(spk_gain)[:, None, :]).reshape(B * L, H)
    xn = f64(normed)
    m1 = np.mean(dn, axis=1, keepdims=True)
    m2 = np.mean(dn * xn, axis=1, keepdims=True)
    dz = f64(inv_std)[:, None] * (dn - m1 - xn * m2)
    a, b = f64(pre_a), f64(pre_b)
    da = dz * sigmoid(b) * (4.0 * sigmoid(2.0 * a) * sigmoid(-2.0 * a)) * f64(gain_a)
    db = dz * np.tanh(a) * (sigmoid(b) * sigmoid(-b)) * f64(gain_b)
    ga = mxq(da, 1, "e5m2") @ mxq(f64(dir_a), 0, "e4m3")
    gb = mxq(db, 1, "e5m2") @ mxq(f64(dir_b), 0, "e4m3")
    return ga + gb

@@ -1,0 +1,455 @@
+from contextlib import ExitStack
+
+import concourse.mybir as mybir
+from concourse.masks import make_identity
+
+ROWS, LOGITS, HID, ENC = 2048, 512, 1024, 512
+UTTERANCES = 8
+
+FLOPS = 2 * ROWS * LOGITS * HID + 2 * 2 * ROWS * HID * ENC
+
+F32 = mybir.dt.float32
+BF16 = mybir.dt.bfloat16
+U32 = mybir.dt.uint32
+U8 = mybir.dt.uint8
+E4X4 = mybir.dt.float8_e4m3fn_x4
+E5X4 = mybir.dt.float8_e5m2_x4
+ALU = mybir.AluOpType
+ACT = mybir.ActivationFunctionType
+
+P = 128
+TILES = ROWS // P
+HALF = 512
+NH = HID // HALF
+
+
+def tile_prosody_predictor_backward_f3_kernel(
+    tc, d_logits, head_w, spk_gain, normed, inv_std, pre_a, pre_b, gain_a, gain_b, dir_a, dir_b, out
+):
+    nc = tc.nc
+
+    dl_rows = d_logits.rearrange("(p i) k -> p i k", i=TILES)
+    xn_rows = normed.rearrange("(p i) h -> p i h", i=TILES)
+    a_rows = pre_a.rearrange("(p i) h -> p i h", i=TILES)
+    b_rows = pre_b.rearrange("(p i) h -> p i h", i=TILES)
+    out_rows = out.rearrange("(p i) d -> p i d", i=TILES)
+    head_k = head_w.rearrange("(p t) h -> p t h", t=4)
+    dirs_k = [w.rearrange("(g p t) d -> g p t d", g=NH, t=4) for w in (dir_a, dir_b)]
+
+    with ExitStack() as ctx:
+        keep = ctx.enter_context(tc.tile_pool(name="keep", bufs=1))
+        raws = ctx.enter_context(tc.tile_pool(name="raws", bufs=3))
+        grps = ctx.enter_context(tc.tile_pool(name="grps", bufs=2))
+        ins = ctx.enter_context(tc.tile_pool(name="ins", bufs=3))
+        three = ctx.enter_context(tc.tile_pool(name="three", bufs=3))
+        two = ctx.enter_context(tc.tile_pool(name="two", bufs=2))
+        small = ctx.enter_context(tc.tile_pool(name="small", bufs=4))
+        ps_dh = ctx.enter_context(tc.psum_pool(name="ps_dh", bufs=2))
+        ps_dz = ctx.enter_context(tc.psum_pool(name="ps_dz", bufs=2))
+        ps_in = ctx.enter_context(tc.psum_pool(name="ps_in", bufs=3))
+        ps_out = ctx.enter_context(tc.psum_pool(name="ps_out", bufs=1))
+        ctx.enter_context(tc.manual_schedule())
+
+        ident = keep.tile([P, P], F32, name="ident")
+        zero_col = keep.tile([P, 1], F32, name="zero_col")
+        inv_raw = keep.tile([P, TILES], BF16, name="inv_raw")
+        inv = keep.tile([P, TILES], F32, name="inv")
+        ga_raw = keep.tile([P, NH, 4], BF16, name="ga_raw")
+        gb_raw = keep.tile([P, NH, 4], BF16, name="gb_raw")
+        ga = keep.tile([P, 8], F32, name="ga")
+        nga = keep.tile([P, 8], F32, name="nga")
+        gb = keep.tile([P, 8], F32, name="gb")
+        sg_raw = keep.tile([P, HID], BF16, name="sg_raw")
+        sg = keep.tile([P, HID], BF16, name="sg")
+        head_codes = keep.tile([P, HID], U32, name="head_codes", align_bytes=64)
+        head_scales = keep.tile([P, HID], U8, name="head_scales", align_bytes=64)
+        dir_codes = keep.tile([P, 4, ENC], U32, name="dir_codes", align_bytes=64)
+        dir_scales = keep.tile([P, 4, ENC], U8, name="dir_scales", align_bytes=64)
+
+        dl_sb, a_sb, b_sb, xn_sb = {}, {}, {}, {}
+        raw_sb = {}
+        dl_ps, dl_grp, dl_codes, dl_scales = {}, {}, {}, {}
+        a_ps, b_ps, dh_ps, dz_ps, out_ps = {}, {}, {}, {}, {}
+        th, sb, sn, sq = {}, {}, {}, {}
+        dn, y, q, sums, means = {}, {}, {}, {}, {}
+        dab, codes, scales, out_sb = {}, {}, {}, {}
+
+        def load_dl(pair):
+            t = ins.tile([P, 2, LOGITS], BF16, name="dl_sb")
+            nc.sync.dma_start(out=t[:], in_=dl_rows[:, 2 * pair : 2 * pair + 2, :])
+            dl_sb[pair] = t
+
+        def load_ab(pair):
+            ta = ins.tile([P, 2, HID], BF16, name="a_sb")
+            nc.sync.dma_start(out=ta[:], in_=a_rows[:, 2 * pair : 2 * pair + 2, :])
+            a_sb[pair] = ta
+            tb = ins.tile([P, 2, HID], BF16, name="b_sb")
+            nc.sync.dma_start(out=tb[:], in_=b_rows[:, 2 * pair : 2 * pair + 2, :])
+            b_sb[pair] = tb
+
+        def load_xn(pair):
+            t = ins.tile([P, 2, HID], BF16, name="xn_sb")
+            nc.sync.dma_start(out=t[:], in_=xn_rows[:, 2 * pair : 2 * pair + 2, :])
+            xn_sb[pair] = t
+
+        def load_raw(key, view):
+            t = raws.tile([P, 4, HALF], BF16, name="raw_sb")
+            nc.sync.dma_start(out=t[:], in_=view)
+            raw_sb[key] = t
+
+        def head_half(g, on_scalar):
+            grouped = grps.tile([P, HALF, 4], BF16, name="grouped", align_bytes=64)
+            dst = grouped[:].rearrange("p (j m) t -> p j m t", j=4)
+            src = raw_sb["head", g][:].rearrange("p t (m j) -> p j m t", j=4)
+            if on_scalar:
+                nc.scalar.copy(out=dst, in_=src)
+            else:
+                nc.vector.tensor_copy(out=dst, in_=src)
+            cols = slice(g * HALF, (g + 1) * HALF)
+            nc.vector.quantize_mx(
+                out=head_codes[:, cols].bitcast(E4X4),
+                scales=head_scales[:, cols],
+                in_=grouped[:].rearrange("p c t -> p (c t)"),
+            )
+
+        dir_grouped = {}
+
+        def dir_group(k):
+            grouped = grps.tile([P, HALF, 4], BF16, name="grouped", align_bytes=64)
+            dst = grouped[:].rearrange("p (c i) t -> p c t i", i=4)
+            src = raw_sb["dir", k][:].rearrange("p t (c i) -> p c t i", i=4)
+            nc.gpsimd.tensor_scalar(
+                out=dst, in0=src, scalar1=1.0, scalar2=0.0, op0=ALU.mult, op1=ALU.add
+            )
+            dir_grouped[k] = grouped
+
+        def dir_quant(k):
+            nc.vector.quantize_mx(
+                out=dir_codes[:, k, :].bitcast(E4X4),
+                scales=dir_scales[:, k, :],
+                in_=dir_grouped[k][:].rearrange("p c t -> p (c t)"),
+            )
+
+        def dl_turn(pair):
+            t = ps_in.tile([P, 512], F32, name="in_ps")
+            words = dl_sb[pair][:].bitcast(F32)
+            for r in range(2):
+                for u in range(2):
+                    s = 2 * r + u
+                    nc.tensor.transpose(
+                        t[:, s * P : (s + 1) * P], words[:, r, u : LOGITS // 2 : 2], ident[:]
+                    )
+            dl_ps[pair] = t
+
+        def dl_copy(pair):
+            grouped = two.tile([P, 2 * P * 4], BF16, name="dl_grp", align_bytes=64)
+            nc.scalar.copy(
+                out=grouped[:].bitcast(F32).rearrange("p (i r u) -> p i r u", i=2, u=2),
+                in_=dl_ps[pair][:].rearrange("p (i u r) -> p i r u", i=2, u=2),
+            )
+            dl_grp[pair] = grouped
+
+        def dl_quant(pair):
+            c = three.tile([P, 2 * P], U32, name="dl_codes", align_bytes=64)
+            s = three.tile([P, 2 * P], U8, name="dl_scales", align_bytes=64)
+            nc.vector.quantize_mx(out=c[:].bitcast(E4X4), scales=s[:], in_=dl_grp[pair][:])
+            dl_codes[pair], dl_scales[pair] = c, s
+
+        def turn_in(i, src, ps):
+            t = ps_in.tile([P, 512], F32, name="in_ps")
+            words = src[i // 2][:].bitcast(F32)
+            for g in range(NH):
+                for u in range(2):
+                    s = 2 * g + u
+                    nc.tensor.transpose(
+                        t[:, s * P : (s + 1) * P],
+                        words[:, i % 2, 256 * g + u : 256 * (g + 1) : 2],
+                        ident[:],
+                    )
+            ps[i] = t
+
+        def act(dst, i, ps, func, scale):
+            rows = slice(P * (i % 2), P * (i % 2 + 1))
+            nc.scalar.activation(
+                out=dst[i // 2][:, :, rows].rearrange("p (s e) r -> p s e r", e=2),
+                in_=ps[i][:].bitcast(BF16).rearrange("p (s r e) -> p s e r", s=4, e=2),
+                func=func,
+                scale=scale,
+            )
+
+        def act_a(i):
+            if i % 2 == 0:
+                th_t = two.tile([P, 8, 2 * P], F32, name="th")
+                sq_t = three.tile([P, 8, 2 * P], F32, name="sq")
+                th[i // 2], sq[i // 2] = th_t, sq_t
+            rows = slice(P * (i % 2), P * (i % 2 + 1))
+            act(th, i, a_ps, ACT.Tanh, 1.0)
+            nc.scalar.activation(
+                out=sq[i // 2][:, :, rows], in_=th[i // 2][:, :, rows], func=ACT.Square
+            )
+
+        def act_b(i):
+            if i % 2 == 0:
+                sb_t = three.tile([P, 8, 2 * P], F32, name="sb")
+                sn_t = three.tile([P, 8, 2 * P], F32, name="sn")
+                sb[i // 2], sn[i // 2] = sb_t, sn_t
+            act(sb, i, b_ps, ACT.Sigmoid, 1.0)
+            act(sn, i, b_ps, ACT.Sigmoid, -1.0)
+
+        def factor_a(pair, part):
+            for s in range(4 * part, 4 * part + 4):
+                nc.gpsimd.tensor_scalar(
+                    out=sq[pair][:, s, :],
+                    in0=sq[pair][:, s, :],
+                    scalar1=nga[:, s : s + 1],
+                    scalar2=ga[:, s : s + 1],
+                    op0=ALU.mult,
+                    op1=ALU.add,
+                )
+
+        def factor_b(pair, s):
+            nc.vector.scalar_tensor_tensor(
+                out=sn[pair][:, s, :],
+                in0=th[pair][:, s, :],
+                scalar=gb[:, s : s + 1],
+                in1=sn[pair][:, s, :],
+                op0=ALU.mult,
+                op1=ALU.mult,
+            )
+
+        def stage1(i):
+            cols = slice(P * (i % 2), P * (i % 2 + 1))
+            for g in range(NH):
+                t = ps_dh.tile([P, HALF], F32, name="dh_ps")
+                h = slice(g * HALF, (g + 1) * HALF)
+                nc.tensor.matmul_mx(
+                    out=t[:],
+                    lhsT=dl_codes[i // 2][:, cols].bitcast(E4X4),
+                    lhsT_scale=dl_scales[i // 2][:, cols],
+                    rhs=head_codes[:, h].bitcast(E4X4),
+                    rhs_scale=head_scales[:, h],
+                    start=True,
+                    stop=True,
+                )
+                dh_ps[i, g] = t
+
+        def norm_1(i, g):
+            if g == 0:
+                dn_t = two.tile([P, HID], F32, name="dn")
+                s_t = small.tile([P, 4], F32, name="sums")
+                dn[i], sums[i] = dn_t, s_t
+            h = slice(g * HALF, (g + 1) * HALF)
+            nc.vector.scalar_tensor_tensor(
+                out=dn[i][:, h],
+                in0=dh_ps[i, g][:],
+                scalar=inv[:, i : i + 1],
+                in1=sg[:, h],
+                op0=ALU.mult,
+                op1=ALU.mult,
+                accum_out=sums[i][:, 2 * g : 2 * g + 1],
+            )
+
+        def norm_2(i, g):
+            h = slice(g * HALF, (g + 1) * HALF)
+            junk = two.tile([P, HALF], F32, name="junk")
+            nc.vector.scalar_tensor_tensor(
+                out=junk[:].rearrange("p (j m) -> p j m", j=4),
+                in0=dn[i][:, h].rearrange("p (j m) -> p j m", j=4),
+                scalar=1.0,
+                in1=xn_sb[i // 2][:, i % 2, h].rearrange("p (m j) -> p j m", j=4),
+                op0=ALU.mult,
+                op1=ALU.mult,
+                accum_out=sums[i][:, 2 * g + 1 : 2 * g + 2],
+            )
+
+        def means_add(i):
+            t = small.tile([P, 2], F32, name="sum2")
+            nc.vector.tensor_tensor(out=t[:], in0=sums[i][:, 0:2], in1=sums[i][:, 2:4], op=ALU.add)
+            means[i] = t
+
+        def means_scale(i):
+            t = small.tile([P, 2], F32, name="mean2")
+            nc.vector.tensor_scalar(
+                out=t[:], in0=means[i][:], scalar1=-1.0 / HID, scalar2=None, op0=ALU.mult
+            )
+            means[i] = t
+
+        def correction(i):
+            t = two.tile([P, HID], F32, name="y")
+            nc.gpsimd.tensor_scalar(
+                out=t[:].rearrange("p (g j m) -> p g j m", g=NH, j=4),
+                in0=xn_sb[i // 2][:, i % 2, :].rearrange("p (g m j) -> p g j m", g=NH, j=4),
+                scalar1=means[i][:, 1:2],
+                scalar2=means[i][:, 0:1],
+                op0=ALU.mult,
+                op1=ALU.add,
+            )
+            y[i] = t
+
+        def turn_dz(i, g):
+            t = ps_dz.tile([P, HALF], F32, name="dz_ps")
+            for j in range(4):
+                s = slice(g * HALF + j * P, g * HALF + (j + 1) * P)
+                o = t[:, j * P : (j + 1) * P]
+                nc.tensor.matmul(o, dn[i][:, s], ident[:], start=True, stop=False, is_transpose=True)
+                nc.tensor.matmul(o, y[i][:, s], ident[:], start=False, stop=True, is_transpose=True)
+            dz_ps[i, g] = t
+
+        def gate(i, g):
+            if g == 0:
+                t = two.tile([P, 8, P], F32, name="q")
+                q[i] = t
+            rows = slice(P * (i % 2), P * (i % 2 + 1))
+            nc.vector.tensor_tensor(
+                out=q[i][:, 4 * g : 4 * g + 4, :],
+                in0=dz_ps[i, g][:].rearrange("p (j r) -> p j r", j=4),
+                in1=sb[i // 2][:, 4 * g : 4 * g + 4, rows],
+                op=ALU.mult,
+            )
+
+        def branch(i, which, g):
+            if which == 0 and g == 0:
+                t = two.tile([P, 2 * NH * 4 * P], BF16, name="dab", align_bytes=64)
+                dab[i] = t
+            rows = slice(P * (i % 2), P * (i % 2 + 1))
+            factor = (sq, sn)[which][i // 2]
+            at = (which * NH + g) * HALF
+            nc.vector.tensor_tensor(
+                out=dab[i][:, at : at + HALF].rearrange("p (c i j) -> p c j i", i=4, j=4),
+                in0=q[i][:, 4 * g : 4 * g + 4, :].rearrange("p j (c i) -> p c j i", i=4),
+                in1=factor[:, 4 * g : 4 * g + 4, rows].rearrange("p j (c i) -> p c j i", i=4),
+                op=ALU.mult,
+            )
+
+        def quant(i):
+            c = two.tile([P, 4 * P], U32, name="codes", align_bytes=64)
+            s = two.tile([P, 4 * P], U8, name="scales", align_bytes=64)
+            nc.vector.quantize_mx(out=c[:].bitcast(E5X4), scales=s[:], in_=dab[i][:])
+            codes[i], scales[i] = c, s
+
+        def stage2(i):
+            t = ps_out.tile([P, ENC], F32, name="out_ps")
+            for k in range(4):
+                cols = slice(k * P, (k + 1) * P)
+                nc.tensor.matmul_mx(
+                    out=t[:],
+                    lhsT=codes[i][:, cols].bitcast(E5X4),
+                    lhsT_scale=scales[i][:, cols],
+                    rhs=dir_codes[:, k, :].bitcast(E4X4),
+                    rhs_scale=dir_scales[:, k, :],
+                    start=(k == 0),
+                    stop=(k == 3),
+                )
+            out_ps[i] = t
+
+        def finish(i):
+            t = three.tile([P, ENC], F32, name="out_sb")
+            nc.scalar.copy(out=t[:], in_=out_ps[i][:])
+            nc.sync.dma_start(out=out_rows[:, i, :], in_=t[:])
+
+        nc.vector.memset(zero_col[:], 0.0)
+        make_identity(nc, ident[:])
+        nc.scalar.dma_start(out=inv_raw[:], in_=inv_std.rearrange("(p i) -> p i", i=TILES))
+        for u in range(UTTERANCES):
+            nc.scalar.dma_start(
+                out=sg_raw[16 * u : 16 * (u + 1), :], in_=spk_gain[u, :].partition_broadcast(16)
+            )
+        nc.scalar.dma_start(out=ga_raw[:], in_=gain_a.rearrange("(g p j) -> p g j", g=NH, j=4))
+        nc.scalar.dma_start(out=gb_raw[:], in_=gain_b.rearrange("(g p j) -> p g j", g=NH, j=4))
+        warm = small.tile([P, 1], F32, name="warm")
+        nc.scalar.activation(out=warm[:], in_=zero_col[:], func=ACT.Sigmoid)
+
+        load_dl(0)
+        for g in range(NH):
+            load_raw(("head", g), head_k[:, :, g * HALF : (g + 1) * HALF])
+        load_ab(0)
+        load_xn(0)
+        load_dl(1)
+        load_ab(1)
+        load_xn(1)
+        for k in range(4):
+            load_raw(("dir", k), dirs_k[k // NH][k % NH])
+        load_dl(2)
+        load_ab(2)
+        load_xn(2)
+
+        def ok(i):
+            return 0 <= i < TILES
+
+        for i in range(-6, TILES + 1):
+            even = i % 2 == 0
+            if not even and 3 <= (i + 9) // 2 < TILES // 2:
+                load_dl((i + 9) // 2)
+                load_ab((i + 9) // 2)
+            if even and 3 <= (i + 6) // 2 < TILES // 2:
+                load_xn((i + 6) // 2)
+
+            if i == -6:
+                nc.vector.tensor_copy(out=inv[:], in_=inv_raw[:])
+                for g in range(NH):
+                    h = slice(g * HALF, (g + 1) * HALF)
+                    nc.vector.tensor_copy(
+                        out=sg[:, h].rearrange("p (j m) -> p j m", j=4),
+                        in_=sg_raw[:, h].rearrange("p (m j) -> p j m", j=4),
+                    )
+                ga_view = ga_raw[:].rearrange("p g j -> p (g j)")
+                nc.vector.tensor_copy(out=ga[:], in_=ga_view)
+                nc.vector.tensor_scalar(out=nga[:], in0=ga_view, scalar1=-1.0, scalar2=None, op0=ALU.mult)
+                nc.vector.tensor_copy(out=gb[:], in_=gb_raw[:].rearrange("p g j -> p (g j)"))
+                head_half(0, False)
+                head_half(1, True)
+            if not even and ok(i + 5):
+                dl_quant((i + 5) // 2)
+            fpair = (i + 2) // 2
+            fb = []
+            if 0 <= fpair < TILES // 2:
+                fb = [(fpair, s) for s in range(4 * (i % 2), 4 * (i % 2) + 4)]
+                factor_a(fpair, i % 2)
+            if ok(i + 2):
+                norm_1(i + 2, 0)
+                norm_1(i + 2, 1)
+            if ok(i - 1):
+                quant(i - 1)
+            if ok(i + 4):
+                act_a(i + 4)
+            if ok(i + 3):
+                stage1(i + 3)
+            if ok(i - 1):
+                stage2(i - 1)
+                finish(i - 1)
+            if even and ok(i + 6):
+                dl_turn((i + 6) // 2)
+                dl_copy((i + 6) // 2)
+            if ok(i + 4):
+                act_b(i + 4)
+            if ok(i + 5):
+                turn_in(i + 5, a_sb, a_ps)
+                turn_in(i + 5, b_sb, b_ps)
+            if ok(i + 1):
+                gate(i + 1, 0)
+            if ok(i + 2):
+                norm_2(i + 2, 0)
+                norm_2(i + 2, 1)
+            if ok(i + 1):
+                gate(i + 1, 1)
+            if ok(i + 2):
+                means_add(i + 2)
+            for f in fb[:1]:
+                factor_b(*f)
+            if ok(i + 2):
+                means_scale(i + 2)
+                correction(i + 2)
+                turn_dz(i + 2, 0)
+                turn_dz(i + 2, 1)
+            for f in fb[1:]:
+                factor_b(*f)
+            if ok(i):
+                for which in range(2):
+                    for g in range(NH):
+                        branch(i, which, g)
+            if i in (-2, -1):
+                dir_group(2 * (i + 2))
+                dir_group(2 * (i + 2) + 1)
+            if i in (-1, 0):
+                dir_quant(2 * (i + 1))
+                dir_quant(2 * (i + 1) + 1)

@@ -19,6 +19,9 @@ ACT = mybir.ActivationFunctionType
 
 P = 128
 TILES = ROWS // P
+EB = {-2: (), -1: range(8)}
+DIRG = {-3: (0,), -2: (1, 2), -1: (3,)}
+DIRQ = {-2: (0,), -1: (1, 2), 0: (3,)}
 HALF = 512
 NH = HID // HALF
 
@@ -39,7 +42,7 @@ def tile_prosody_predictor_backward_f3_kernel(
     with ExitStack() as ctx:
         keep = ctx.enter_context(tc.tile_pool(name="keep", bufs=1))
         raws = ctx.enter_context(tc.tile_pool(name="raws", bufs=3))
-        grps = ctx.enter_context(tc.tile_pool(name="grps", bufs=2))
+        grps = ctx.enter_context(tc.tile_pool(name="grps", bufs=3))
         ins = ctx.enter_context(tc.tile_pool(name="ins", bufs=3))
         three = ctx.enter_context(tc.tile_pool(name="three", bufs=3))
         two = ctx.enter_context(tc.tile_pool(name="two", bufs=2))
@@ -71,7 +74,7 @@ def tile_prosody_predictor_backward_f3_kernel(
         dl_ps, dl_grp, dl_codes, dl_scales = {}, {}, {}, {}
         a_ps, b_ps, dh_ps, dz_ps, out_ps = {}, {}, {}, {}, {}
         th, sb, sn, sq = {}, {}, {}, {}
-        dn, y, q, sums, means = {}, {}, {}, {}, {}
+        dn, y, q, sums = {}, {}, {}, {}
         dab, codes, scales, out_sb = {}, {}, {}, {}
 
         def load_dl(pair):
@@ -80,9 +83,15 @@ def tile_prosody_predictor_backward_f3_kernel(
             dl_sb[pair] = t
 
         def load_ab(pair):
+            load_b(pair)
+            load_a(pair)
+
+        def load_a(pair):
             ta = ins.tile([P, 2, HID], BF16, name="a_sb")
             nc.sync.dma_start(out=ta[:], in_=a_rows[:, 2 * pair : 2 * pair + 2, :])
             a_sb[pair] = ta
+
+        def load_b(pair):
             tb = ins.tile([P, 2, HID], BF16, name="b_sb")
             nc.sync.dma_start(out=tb[:], in_=b_rows[:, 2 * pair : 2 * pair + 2, :])
             b_sb[pair] = tb
@@ -97,19 +106,22 @@ def tile_prosody_predictor_backward_f3_kernel(
             nc.sync.dma_start(out=t[:], in_=view)
             raw_sb[key] = t
 
-        def head_half(g, on_scalar):
+        head_grouped = {}
+
+        def head_group(g):
             grouped = grps.tile([P, HALF, 4], BF16, name="grouped", align_bytes=64)
-            dst = grouped[:].rearrange("p (j m) t -> p j m t", j=4)
-            src = raw_sb["head", g][:].rearrange("p t (m j) -> p j m t", j=4)
-            if on_scalar:
-                nc.scalar.copy(out=dst, in_=src)
-            else:
-                nc.vector.tensor_copy(out=dst, in_=src)
-            cols = slice(g * HALF, (g + 1) * HALF)
+            nc.vector.tensor_copy(
+                out=grouped[:].rearrange("p (j m) t -> p j m t", j=4),
+                in_=raw_sb["head", g][:].rearrange("p t (m j) -> p j m t", j=4),
+            )
+            head_grouped[g] = grouped
+
+        def head_quant(g, j):
+            at = (j * NH + g) * P
             nc.vector.quantize_mx(
-                out=head_codes[:, cols].bitcast(E4X4),
-                scales=head_scales[:, cols],
-                in_=grouped[:].rearrange("p c t -> p (c t)"),
+                out=head_codes[:, at : at + P].bitcast(E4X4),
+                scales=head_scales[:, at : at + P],
+                in_=head_grouped[g][:, j * P : (j + 1) * P, :].rearrange("p c t -> p (c t)"),
             )
 
         dir_grouped = {}
@@ -118,9 +130,7 @@ def tile_prosody_predictor_backward_f3_kernel(
             grouped = grps.tile([P, HALF, 4], BF16, name="grouped", align_bytes=64)
             dst = grouped[:].rearrange("p (c i) t -> p c t i", i=4)
             src = raw_sb["dir", k][:].rearrange("p t (c i) -> p c t i", i=4)
-            nc.gpsimd.tensor_scalar(
-                out=dst, in0=src, scalar1=1.0, scalar2=0.0, op0=ALU.mult, op1=ALU.add
-            )
+            nc.vector.tensor_copy(out=dst, in_=src)
             dir_grouped[k] = grouped
 
         def dir_quant(k):
@@ -198,13 +208,12 @@ def tile_prosody_predictor_backward_f3_kernel(
 
         def factor_a(pair, part):
             for s in range(4 * part, 4 * part + 4):
-                nc.gpsimd.tensor_scalar(
+                nc.scalar.activation(
                     out=sq[pair][:, s, :],
-                    in0=sq[pair][:, s, :],
-                    scalar1=nga[:, s : s + 1],
-                    scalar2=ga[:, s : s + 1],
-                    op0=ALU.mult,
-                    op1=ALU.add,
+                    in_=sq[pair][:, s, :],
+                    func=ACT.Identity,
+                    scale=nga[:, s : s + 1],
+                    bias=ga[:, s : s + 1],
                 )
 
         def factor_b(pair, s):
@@ -246,41 +255,38 @@ def tile_prosody_predictor_backward_f3_kernel(
                 in1=sg[:, h],
                 op0=ALU.mult,
                 op1=ALU.mult,
-                accum_out=sums[i][:, 2 * g : 2 * g + 1],
+                accum_out=sums[i][:, g : g + 1],
             )
 
-        def norm_2(i, g):
-            h = slice(g * HALF, (g + 1) * HALF)
-            junk = two.tile([P, HALF], F32, name="junk")
+        def norm_2(i):
+            junk = two.tile([P, HID], F32, name="junk")
             nc.vector.scalar_tensor_tensor(
-                out=junk[:].rearrange("p (j m) -> p j m", j=4),
-                in0=dn[i][:, h].rearrange("p (j m) -> p j m", j=4),
-                scalar=1.0,
-                in1=xn_sb[i // 2][:, i % 2, h].rearrange("p (m j) -> p j m", j=4),
+                out=junk[:].rearrange("p (j q) -> p j q", j=4),
+                in0=dn[i][:].rearrange("p (j q) -> p j q", j=4),
+                scalar=-1.0 / HID,
+                in1=xn_sb[i // 2][:, i % 2, :].rearrange("p (q j) -> p j q", j=4),
                 op0=ALU.mult,
                 op1=ALU.mult,
-                accum_out=sums[i][:, 2 * g + 1 : 2 * g + 2],
+                accum_out=sums[i][:, 2:3],
             )
 
-        def means_add(i):
-            t = small.tile([P, 2], F32, name="sum2")
-            nc.vector.tensor_tensor(out=t[:], in0=sums[i][:, 0:2], in1=sums[i][:, 2:4], op=ALU.add)
-            means[i] = t
-
-        def means_scale(i):
-            t = small.tile([P, 2], F32, name="mean2")
+        def mean_1(i):
             nc.vector.tensor_scalar(
-                out=t[:], in0=means[i][:], scalar1=-1.0 / HID, scalar2=None, op0=ALU.mult
+                out=sums[i][:, 3:4],
+                in0=sums[i][:, 0:1],
+                scalar1=sums[i][:, 1:2],
+                scalar2=-1.0 / HID,
+                op0=ALU.add,
+                op1=ALU.mult,
             )
-            means[i] = t
 
         def correction(i):
             t = two.tile([P, HID], F32, name="y")
             nc.gpsimd.tensor_scalar(
-                out=t[:].rearrange("p (g j m) -> p g j m", g=NH, j=4),
-                in0=xn_sb[i // 2][:, i % 2, :].rearrange("p (g m j) -> p g j m", g=NH, j=4),
-                scalar1=means[i][:, 1:2],
-                scalar2=means[i][:, 0:1],
+                out=t[:].rearrange("p (j q) -> p j q", j=4),
+                in0=xn_sb[i // 2][:, i % 2, :].rearrange("p (q j) -> p j q", j=4),
+                scalar1=sums[i][:, 2:3],
+                scalar2=sums[i][:, 3:4],
                 op0=ALU.mult,
                 op1=ALU.add,
             )
@@ -289,7 +295,7 @@ def tile_prosody_predictor_backward_f3_kernel(
         def turn_dz(i, g):
             t = ps_dz.tile([P, HALF], F32, name="dz_ps")
             for j in range(4):
-                s = slice(g * HALF + j * P, g * HALF + (j + 1) * P)
+                s = slice((j * NH + g) * P, (j * NH + g + 1) * P)
                 o = t[:, j * P : (j + 1) * P]
                 nc.tensor.matmul(o, dn[i][:, s], ident[:], start=True, stop=False, is_transpose=True)
                 nc.tensor.matmul(o, y[i][:, s], ident[:], start=False, stop=True, is_transpose=True)
@@ -362,21 +368,42 @@ def tile_prosody_predictor_backward_f3_kernel(
         load_dl(0)
         for g in range(NH):
             load_raw(("head", g), head_k[:, :, g * HALF : (g + 1) * HALF])
-        load_ab(0)
+        load_b(0)
         load_xn(0)
+        load_a(0)
         load_dl(1)
-        load_ab(1)
-        load_xn(1)
         for k in range(4):
             load_raw(("dir", k), dirs_k[k // NH][k % NH])
+        load_b(1)
+        load_a(1)
+        load_xn(1)
         load_dl(2)
         load_ab(2)
         load_xn(2)
 
+        nc.vector.tensor_copy(out=inv[:], in_=inv_raw[:])
+        nc.vector.tensor_copy(
+            out=sg[:].rearrange("p (j q) -> p j q", j=4),
+            in_=sg_raw[:].rearrange("p (q j) -> p j q", j=4),
+        )
+        ga_view = ga_raw[:].rearrange("p g j -> p (g j)")
+        nc.vector.tensor_copy(out=ga[:], in_=ga_view)
+        nc.vector.tensor_scalar(out=nga[:], in0=ga_view, scalar1=-1.0, scalar2=None, op0=ALU.mult)
+        nc.vector.tensor_copy(out=gb[:], in_=gb_raw[:].rearrange("p g j -> p (g j)"))
+        dl_turn(0)
+        dl_copy(0)
+        head_group(0)
+        dl_quant(0)
+        head_group(1)
+        for j in range(4):
+            for g in range(NH):
+                head_quant(g, j)
+        stage1(0)
+
         def ok(i):
             return 0 <= i < TILES
 
-        for i in range(-6, TILES + 1):
+        for i in range(-5, TILES):
             even = i % 2 == 0
             if not even and 3 <= (i + 9) // 2 < TILES // 2:
                 load_dl((i + 9) // 2)
@@ -384,72 +411,59 @@ def tile_prosody_predictor_backward_f3_kernel(
             if even and 3 <= (i + 6) // 2 < TILES // 2:
                 load_xn((i + 6) // 2)
 
-            if i == -6:
-                nc.vector.tensor_copy(out=inv[:], in_=inv_raw[:])
-                for g in range(NH):
-                    h = slice(g * HALF, (g + 1) * HALF)
-                    nc.vector.tensor_copy(
-                        out=sg[:, h].rearrange("p (j m) -> p j m", j=4),
-                        in_=sg_raw[:, h].rearrange("p (m j) -> p j m", j=4),
-                    )
-                ga_view = ga_raw[:].rearrange("p g j -> p (g j)")
-                nc.vector.tensor_copy(out=ga[:], in_=ga_view)
-                nc.vector.tensor_scalar(out=nga[:], in0=ga_view, scalar1=-1.0, scalar2=None, op0=ALU.mult)
-                nc.vector.tensor_copy(out=gb[:], in_=gb_raw[:].rearrange("p g j -> p (g j)"))
-                head_half(0, False)
-                head_half(1, True)
-            if not even and ok(i + 5):
-                dl_quant((i + 5) // 2)
-            fpair = (i + 2) // 2
-            fb = []
-            if 0 <= fpair < TILES // 2:
-                fb = [(fpair, s) for s in range(4 * (i % 2), 4 * (i % 2) + 4)]
-                factor_a(fpair, i % 2)
-            if ok(i + 2):
-                norm_1(i + 2, 0)
-                norm_1(i + 2, 1)
-            if ok(i - 1):
-                quant(i - 1)
-            if ok(i + 4):
-                act_a(i + 4)
-            if ok(i + 3):
-                stage1(i + 3)
-            if ok(i - 1):
-                stage2(i - 1)
-                finish(i - 1)
-            if even and ok(i + 6):
-                dl_turn((i + 6) // 2)
-                dl_copy((i + 6) // 2)
-            if ok(i + 4):
-                act_b(i + 4)
-            if ok(i + 5):
-                turn_in(i + 5, a_sb, a_ps)
-                turn_in(i + 5, b_sb, b_ps)
-            if ok(i + 1):
-                gate(i + 1, 0)
-            if ok(i + 2):
-                norm_2(i + 2, 0)
-                norm_2(i + 2, 1)
-            if ok(i + 1):
-                gate(i + 1, 1)
-            if ok(i + 2):
-                means_add(i + 2)
-            for f in fb[:1]:
-                factor_b(*f)
-            if ok(i + 2):
-                means_scale(i + 2)
-                correction(i + 2)
-                turn_dz(i + 2, 0)
-                turn_dz(i + 2, 1)
-            for f in fb[1:]:
-                factor_b(*f)
             if ok(i):
                 for which in range(2):
                     for g in range(NH):
                         branch(i, which, g)
-            if i in (-2, -1):
-                dir_group(2 * (i + 2))
-                dir_group(2 * (i + 2) + 1)
-            if i in (-1, 0):
-                dir_quant(2 * (i + 1))
-                dir_quant(2 * (i + 1) + 1)
+            if ok(i + 2):
+                norm_2(i + 2)
+            if even and i > -4 and ok(i + 4):
+                dl_quant((i + 4) // 2)
+            if i in DIRQ:
+                for k in DIRQ[i]:
+                    dir_quant(k)
+            if ok(i):
+                quant(i)
+
+            if ok(i + 4):
+                act_b(i + 4)
+            if ok(i + 3) and i >= 0:
+                stage1(i + 3)
+            if ok(i):
+                stage2(i)
+            if even and ok(i + 6):
+                dl_copy((i + 6) // 2)
+            if ok(i + 4):
+                act_a(i + 4)
+            fpair = (i + 2) // 2
+            if 0 <= fpair < TILES // 2:
+                factor_a(fpair, i % 2)
+            if ok(i):
+                finish(i)
+
+            if ok(i + 1):
+                gate(i + 1, 0)
+            if ok(i + 2):
+                mean_1(i + 2)
+                correction(i + 2)
+                turn_dz(i + 2, 0)
+            if ok(i + 1):
+                gate(i + 1, 1)
+            if ok(i + 2):
+                turn_dz(i + 2, 1)
+            if ok(i + 3):
+                norm_1(i + 3, 0)
+                norm_1(i + 3, 1)
+            if i in (-3, -2):
+                stage1(i + 4)
+            if ok(i + 5):
+                turn_in(i + 5, b_sb, b_ps)
+                turn_in(i + 5, a_sb, a_ps)
+            if not even and ok(i + 7):
+                dl_turn((i + 7) // 2)
+            if 0 <= fpair < TILES // 2:
+                for s in EB.get(i, range(4 * (i % 2), 4 * (i % 2) + 4)):
+                    factor_b(fpair, s)
+            if i in DIRG:
+                for k in DIRG[i]:
+                    dir_group(k)

@@ -19,9 +19,8 @@ ACT = mybir.ActivationFunctionType
 
 P = 128
 TILES = ROWS // P
-EB = {-2: (), -1: range(8)}
-DIRG = {-3: (0,), -2: (1, 2), -1: (3,)}
-DIRQ = {-2: (0,), -1: (1, 2), 0: (3,)}
+NG = 4
+CV = (0, 1, 2, 3)
 HALF = 512
 NH = HID // HALF
 
@@ -62,12 +61,15 @@ def tile_prosody_predictor_backward_f3_kernel(
         ga = keep.tile([P, 8], F32, name="ga")
         nga = keep.tile([P, 8], F32, name="nga")
         gb = keep.tile([P, 8], F32, name="gb")
+        ngb = keep.tile([P, 8], F32, name="ngb")
         sg_raw = keep.tile([P, HID], BF16, name="sg_raw")
         sg = keep.tile([P, HID], BF16, name="sg")
         head_codes = keep.tile([P, HID], U32, name="head_codes", align_bytes=64)
         head_scales = keep.tile([P, HID], U8, name="head_scales", align_bytes=64)
         dir_codes = keep.tile([P, 4, ENC], U32, name="dir_codes", align_bytes=64)
         dir_scales = keep.tile([P, 4, ENC], U8, name="dir_scales", align_bytes=64)
+
+        junk = keep.tile([P, HID], F32, name="junk")
 
         dl_sb, a_sb, b_sb, xn_sb = {}, {}, {}, {}
         raw_sb = {}
@@ -204,26 +206,45 @@ def tile_prosody_predictor_backward_f3_kernel(
                 sn_t = three.tile([P, 8, 2 * P], F32, name="sn")
                 sb[i // 2], sn[i // 2] = sb_t, sn_t
             act(sb, i, b_ps, ACT.Sigmoid, 1.0)
-            act(sn, i, b_ps, ACT.Sigmoid, -1.0)
 
-        def factor_a(pair, part):
-            for s in range(4 * part, 4 * part + 4):
+        def affine(dst, src, s, minus, plus, on_vector):
+            if on_vector:
+                nc.vector.tensor_scalar(
+                    out=dst[:, s, :],
+                    in0=src[:, s, :],
+                    scalar1=minus[:, s : s + 1],
+                    scalar2=plus[:, s : s + 1],
+                    op0=ALU.mult,
+                    op1=ALU.add,
+                )
+            else:
                 nc.scalar.activation(
-                    out=sq[pair][:, s, :],
-                    in_=sq[pair][:, s, :],
+                    out=dst[:, s, :],
+                    in_=src[:, s, :],
                     func=ACT.Identity,
-                    scale=nga[:, s : s + 1],
-                    bias=ga[:, s : s + 1],
+                    scale=minus[:, s : s + 1],
+                    bias=plus[:, s : s + 1],
                 )
 
-        def factor_b(pair, s):
-            nc.vector.scalar_tensor_tensor(
-                out=sn[pair][:, s, :],
-                in0=th[pair][:, s, :],
-                scalar=gb[:, s : s + 1],
-                in1=sn[pair][:, s, :],
-                op0=ALU.mult,
-                op1=ALU.mult,
+        def factor_a(pair, s, on_vector):
+            affine(sq[pair], sq[pair], s, nga, ga, on_vector)
+
+        def factor_b(pair, s, on_vector):
+            affine(sn[pair], sb[pair], s, ngb, gb, on_vector)
+
+        def factor_b_tanh(pair, part, i):
+            if i >= 0:
+                tick = small.tile([P, 1], F32, name="tick")
+                nc.gpsimd.tensor_copy(out=tick[:], in_=sums[i][:, 3:4])
+            s = slice(4 * part, 4 * part + NG)
+            nc.gpsimd.tensor_tensor(
+                out=sn[pair][:, s, :], in0=th[pair][:, s, :], in1=sn[pair][:, s, :], op=ALU.mult
+            )
+
+        def factor_b_tanh_v(pair, part):
+            s = slice(4 * part + NG, 4 * part + 4)
+            nc.vector.tensor_tensor(
+                out=sn[pair][:, s, :], in0=th[pair][:, s, :], in1=sn[pair][:, s, :], op=ALU.mult
             )
 
         def stage1(i):
@@ -244,7 +265,7 @@ def tile_prosody_predictor_backward_f3_kernel(
 
         def norm_1(i, g):
             if g == 0:
-                dn_t = two.tile([P, HID], F32, name="dn")
+                dn_t = three.tile([P, HID], F32, name="dn")
                 s_t = small.tile([P, 4], F32, name="sums")
                 dn[i], sums[i] = dn_t, s_t
             h = slice(g * HALF, (g + 1) * HALF)
@@ -259,7 +280,6 @@ def tile_prosody_predictor_backward_f3_kernel(
             )
 
         def norm_2(i):
-            junk = two.tile([P, HID], F32, name="junk")
             nc.vector.scalar_tensor_tensor(
                 out=junk[:].rearrange("p (j q) -> p j q", j=4),
                 in0=dn[i][:].rearrange("p (j q) -> p j q", j=4),
@@ -282,13 +302,12 @@ def tile_prosody_predictor_backward_f3_kernel(
 
         def correction(i):
             t = two.tile([P, HID], F32, name="y")
-            nc.gpsimd.tensor_scalar(
+            nc.scalar.activation(
                 out=t[:].rearrange("p (j q) -> p j q", j=4),
-                in0=xn_sb[i // 2][:, i % 2, :].rearrange("p (q j) -> p j q", j=4),
-                scalar1=sums[i][:, 2:3],
-                scalar2=sums[i][:, 3:4],
-                op0=ALU.mult,
-                op1=ALU.add,
+                in_=xn_sb[i // 2][:, i % 2, :].rearrange("p (q j) -> p j q", j=4),
+                func=ACT.Identity,
+                scale=sums[i][:, 2:3],
+                bias=sums[i][:, 3:4],
             )
             y[i] = t
 
@@ -369,8 +388,8 @@ def tile_prosody_predictor_backward_f3_kernel(
         for g in range(NH):
             load_raw(("head", g), head_k[:, :, g * HALF : (g + 1) * HALF])
         load_b(0)
-        load_xn(0)
         load_a(0)
+        load_xn(0)
         load_dl(1)
         for k in range(4):
             load_raw(("dir", k), dirs_k[k // NH][k % NH])
@@ -389,81 +408,157 @@ def tile_prosody_predictor_backward_f3_kernel(
         ga_view = ga_raw[:].rearrange("p g j -> p (g j)")
         nc.vector.tensor_copy(out=ga[:], in_=ga_view)
         nc.vector.tensor_scalar(out=nga[:], in0=ga_view, scalar1=-1.0, scalar2=None, op0=ALU.mult)
-        nc.vector.tensor_copy(out=gb[:], in_=gb_raw[:].rearrange("p g j -> p (g j)"))
+        gb_view = gb_raw[:].rearrange("p g j -> p (g j)")
+        nc.vector.tensor_copy(out=gb[:], in_=gb_view)
+        nc.vector.tensor_scalar(out=ngb[:], in0=gb_view, scalar1=-1.0, scalar2=None, op0=ALU.mult)
         dl_turn(0)
         dl_copy(0)
         head_group(0)
         dl_quant(0)
+        turn_in(0, b_sb, b_ps)
+        turn_in(0, a_sb, a_ps)
+        act_b(0)
+        act_a(0)
+        turn_in(1, b_sb, b_ps)
         head_group(1)
         for j in range(4):
             for g in range(NH):
                 head_quant(g, j)
         stage1(0)
+        turn_in(1, a_sb, a_ps)
+        act_b(1)
+        act_a(1)
+        norm_1(0, 0)
+        norm_1(0, 1)
+        stage1(1)
+        norm_2(0)
+        norm_1(1, 0)
+        norm_1(1, 1)
+        mean_1(0)
+        correction(0)
+        dl_turn(1)
+        dl_copy(1)
+        norm_2(1)
+        dl_quant(1)
+        mean_1(1)
+        correction(1)
+        turn_dz(0, 0)
+        turn_dz(0, 1)
+        stage1(2)
+        for part in range(2):
+            for s in range(4 * part, 4 * part + 4):
+                affine(sn[0], sb[0], s, ngb, gb, True)
+            for s in range(4 * part, 4 * part + 4):
+                affine(sq[0], sq[0], s, nga, ga, True)
+            factor_b_tanh(0, part, -1)
+        gate(0, 0)
+        gate(0, 1)
+        turn_dz(1, 0)
+        turn_dz(1, 1)
+        dir_group(0)
+        dir_group(1)
+        dir_quant(0)
+        dir_group(2)
+        dir_quant(1)
+        turn_in(2, b_sb, b_ps)
+        turn_in(2, a_sb, a_ps)
+        act_b(2)
+        act_a(2)
+        turn_in(3, b_sb, b_ps)
+        turn_in(3, a_sb, a_ps)
+        act_b(3)
+        act_a(3)
+        dl_turn(2)
+        dl_copy(2)
+        load_dl(3)
+        load_ab(3)
+        load_dl(4)
+        load_ab(4)
+        turn_in(4, b_sb, b_ps)
+        turn_in(4, a_sb, a_ps)
+        dl_turn(3)
+        norm_1(2, 0)
+        norm_1(2, 1)
+        dir_group(3)
+        dir_quant(2)
+        dir_quant(3)
+        for s in range(4):
+            if s not in CV:
+                factor_a(1, s, False)
+            factor_b(1, s, False)
 
         def ok(i):
             return 0 <= i < TILES
 
-        for i in range(-5, TILES):
+        for i in range(TILES):
             even = i % 2 == 0
-            if not even and 3 <= (i + 9) // 2 < TILES // 2:
+            if not even and (i + 9) // 2 < TILES // 2:
                 load_dl((i + 9) // 2)
                 load_ab((i + 9) // 2)
-            if even and 3 <= (i + 6) // 2 < TILES // 2:
+            if even and (i + 6) // 2 < TILES // 2:
                 load_xn((i + 6) // 2)
 
+            n1 = i + 3
+            n2 = i + 2
+            ys = i + 2
+            gt = i + 1
             if ok(i):
                 for which in range(2):
                     for g in range(NH):
                         branch(i, which, g)
-            if ok(i + 2):
-                norm_2(i + 2)
-            if even and i > -4 and ok(i + 4):
+            if ok(n2):
+                norm_2(n2)
+            if even and ok(i + 4):
                 dl_quant((i + 4) // 2)
-            if i in DIRQ:
-                for k in DIRQ[i]:
-                    dir_quant(k)
             if ok(i):
                 quant(i)
 
+            if ok(n2):
+                mean_1(n2)
+
             if ok(i + 4):
                 act_b(i + 4)
-            if ok(i + 3) and i >= 0:
+            if ok(i + 3):
                 stage1(i + 3)
+            if ok(i + 5):
+                turn_in(i + 5, b_sb, b_ps)
+                turn_in(i + 5, a_sb, a_ps)
             if ok(i):
                 stage2(i)
             if even and ok(i + 6):
                 dl_copy((i + 6) // 2)
             if ok(i + 4):
                 act_a(i + 4)
-            fpair = (i + 2) // 2
-            if 0 <= fpair < TILES // 2:
-                factor_a(fpair, i % 2)
-            if ok(i):
-                finish(i)
-
-            if ok(i + 1):
-                gate(i + 1, 0)
-            if ok(i + 2):
-                mean_1(i + 2)
-                correction(i + 2)
-                turn_dz(i + 2, 0)
-            if ok(i + 1):
-                gate(i + 1, 1)
-            if ok(i + 2):
-                turn_dz(i + 2, 1)
-            if ok(i + 3):
-                norm_1(i + 3, 0)
-                norm_1(i + 3, 1)
-            if i in (-3, -2):
-                stage1(i + 4)
-            if ok(i + 5):
-                turn_in(i + 5, b_sb, b_ps)
-                turn_in(i + 5, a_sb, a_ps)
             if not even and ok(i + 7):
                 dl_turn((i + 7) // 2)
+            fpair = (i + 3) // 2
+            part = (i + 3) % 2
             if 0 <= fpair < TILES // 2:
-                for s in EB.get(i, range(4 * (i % 2), 4 * (i % 2) + 4)):
-                    factor_b(fpair, s)
-            if i in DIRG:
-                for k in DIRG[i]:
-                    dir_group(k)
+                for s in range(4 * part, 4 * part + 4):
+                    if s not in CV:
+                        factor_a(fpair, s, False)
+                    factor_b(fpair, s, False)
+            if ok(ys):
+                correction(ys)
+            if ok(i):
+                finish(i)
+            epair = (i + 2) // 2
+            if 0 <= epair < TILES // 2:
+                if NG:
+                    factor_b_tanh(epair, i % 2, i + 2 if 0 <= i < TILES - 2 else -1)
+
+            if ok(gt):
+                gate(gt, 0)
+                gate(gt, 1)
+            if ok(n1):
+                norm_1(n1, 0)
+                norm_1(n1, 1)
+            if ok(ys):
+                turn_dz(ys, 0)
+                turn_dz(ys, 1)
+            if 0 <= epair < TILES // 2 and NG < 4:
+                factor_b_tanh_v(epair, i % 2)
+            if 0 <= epair < TILES // 2:
+                for s in range(4 * (i % 2), 4 * (i % 2) + 4):
+                    if s in CV:
+                        factor_a(epair, s, True)

@@ -20,6 +20,9 @@ ACT = mybir.ActivationFunctionType
 P = 128
 TILES = ROWS // P
 NG = 4
+PLAIN = ()
+DS = (0,)
+DV = (1, 2, 3)
 CV = (0, 1, 2, 3)
 HALF = 512
 NH = HID // HALF
@@ -128,11 +131,14 @@ def tile_prosody_predictor_backward_f3_kernel(
 
         dir_grouped = {}
 
-        def dir_group(k):
+        def dir_group(k, on_scalar):
             grouped = grps.tile([P, HALF, 4], BF16, name="grouped", align_bytes=64)
             dst = grouped[:].rearrange("p (c i) t -> p c t i", i=4)
             src = raw_sb["dir", k][:].rearrange("p t (c i) -> p c t i", i=4)
-            nc.vector.tensor_copy(out=dst, in_=src)
+            if on_scalar:
+                nc.scalar.copy(out=dst, in_=src)
+            else:
+                nc.vector.tensor_copy(out=dst, in_=src)
             dir_grouped[k] = grouped
 
         def dir_quant(k):
@@ -247,10 +253,13 @@ def tile_prosody_predictor_backward_f3_kernel(
                 out=sn[pair][:, s, :], in0=th[pair][:, s, :], in1=sn[pair][:, s, :], op=ALU.mult
             )
 
-        def stage1(i):
+        def stage1(i, fresh=True):
             cols = slice(P * (i % 2), P * (i % 2 + 1))
             for g in range(NH):
-                t = ps_dh.tile([P, HALF], F32, name="dh_ps")
+                if fresh:
+                    t = ps_dh.tile([P, HALF], F32, name="dh_ps")
+                else:
+                    t = dh_ps[i, g]
                 h = slice(g * HALF, (g + 1) * HALF)
                 nc.tensor.matmul_mx(
                     out=t[:],
@@ -316,7 +325,10 @@ def tile_prosody_predictor_backward_f3_kernel(
             for j in range(4):
                 s = slice((j * NH + g) * P, (j * NH + g + 1) * P)
                 o = t[:, j * P : (j + 1) * P]
-                nc.tensor.matmul(o, dn[i][:, s], ident[:], start=True, stop=False, is_transpose=True)
+                if j in PLAIN:
+                    nc.tensor.matmul(o, dn[i][:, s], ident[:], start=True, stop=False)
+                else:
+                    nc.tensor.matmul(o, dn[i][:, s], ident[:], start=True, stop=False, is_transpose=True)
                 nc.tensor.matmul(o, y[i][:, s], ident[:], start=False, stop=True, is_transpose=True)
             dz_ps[i, g] = t
 
@@ -346,11 +358,17 @@ def tile_prosody_predictor_backward_f3_kernel(
                 op=ALU.mult,
             )
 
-        def quant(i):
-            c = two.tile([P, 4 * P], U32, name="codes", align_bytes=64)
-            s = two.tile([P, 4 * P], U8, name="scales", align_bytes=64)
-            nc.vector.quantize_mx(out=c[:].bitcast(E5X4), scales=s[:], in_=dab[i][:])
-            codes[i], scales[i] = c, s
+        def quant(i, which):
+            if which == 0:
+                c = two.tile([P, 4 * P], U32, name="codes", align_bytes=64)
+                s = two.tile([P, 4 * P], U8, name="scales", align_bytes=64)
+                codes[i], scales[i] = c, s
+            half = slice(which * 2 * P, (which + 1) * 2 * P)
+            nc.vector.quantize_mx(
+                out=codes[i][:, half].bitcast(E5X4),
+                scales=scales[i][:, half],
+                in_=dab[i][:, which * HID : (which + 1) * HID],
+            )
 
         def stage2(i):
             t = ps_out.tile([P, ENC], F32, name="out_ps")
@@ -369,8 +387,16 @@ def tile_prosody_predictor_backward_f3_kernel(
 
         def finish(i):
             t = three.tile([P, ENC], F32, name="out_sb")
-            nc.scalar.copy(out=t[:], in_=out_ps[i][:])
-            nc.sync.dma_start(out=out_rows[:, i, :], in_=t[:])
+            if i < TILES - 1:
+                nc.scalar.copy(out=t[:], in_=out_ps[i][:])
+                nc.sync.dma_start(out=out_rows[:, i, :], in_=t[:])
+            else:
+                half = ENC // 2
+                t2 = keep.tile([P, half], F32, name="out_sb2")
+                nc.scalar.copy(out=t[:, :half], in_=out_ps[i][:, :half])
+                nc.sync.dma_start(out=out_rows[:, i, :half], in_=t[:, :half])
+                nc.scalar.copy(out=t2[:], in_=out_ps[i][:, half:])
+                nc.scalar.dma_start(out=out_rows[:, i, half:], in_=t2[:])
 
         nc.vector.memset(zero_col[:], 0.0)
         make_identity(nc, ident[:])
@@ -379,8 +405,6 @@ def tile_prosody_predictor_backward_f3_kernel(
             nc.scalar.dma_start(
                 out=sg_raw[16 * u : 16 * (u + 1), :], in_=spk_gain[u, :].partition_broadcast(16)
             )
-        nc.scalar.dma_start(out=ga_raw[:], in_=gain_a.rearrange("(g p j) -> p g j", g=NH, j=4))
-        nc.scalar.dma_start(out=gb_raw[:], in_=gain_b.rearrange("(g p j) -> p g j", g=NH, j=4))
         warm = small.tile([P, 1], F32, name="warm")
         nc.scalar.activation(out=warm[:], in_=zero_col[:], func=ACT.Sigmoid)
 
@@ -390,8 +414,10 @@ def tile_prosody_predictor_backward_f3_kernel(
         load_b(0)
         load_a(0)
         load_xn(0)
+        nc.sync.dma_start(out=ga_raw[:], in_=gain_a.rearrange("(g p j) -> p g j", g=NH, j=4))
+        nc.sync.dma_start(out=gb_raw[:], in_=gain_b.rearrange("(g p j) -> p g j", g=NH, j=4))
         load_dl(1)
-        for k in range(4):
+        for k in DS + DV:
             load_raw(("dir", k), dirs_k[k // NH][k % NH])
         load_b(1)
         load_a(1)
@@ -400,17 +426,6 @@ def tile_prosody_predictor_backward_f3_kernel(
         load_ab(2)
         load_xn(2)
 
-        nc.vector.tensor_copy(out=inv[:], in_=inv_raw[:])
-        nc.vector.tensor_copy(
-            out=sg[:].rearrange("p (j q) -> p j q", j=4),
-            in_=sg_raw[:].rearrange("p (q j) -> p j q", j=4),
-        )
-        ga_view = ga_raw[:].rearrange("p g j -> p (g j)")
-        nc.vector.tensor_copy(out=ga[:], in_=ga_view)
-        nc.vector.tensor_scalar(out=nga[:], in0=ga_view, scalar1=-1.0, scalar2=None, op0=ALU.mult)
-        gb_view = gb_raw[:].rearrange("p g j -> p (g j)")
-        nc.vector.tensor_copy(out=gb[:], in_=gb_view)
-        nc.vector.tensor_scalar(out=ngb[:], in0=gb_view, scalar1=-1.0, scalar2=None, op0=ALU.mult)
         dl_turn(0)
         dl_copy(0)
         head_group(0)
@@ -425,6 +440,11 @@ def tile_prosody_predictor_backward_f3_kernel(
             for g in range(NH):
                 head_quant(g, j)
         stage1(0)
+        nc.vector.tensor_copy(out=inv[:], in_=inv_raw[:])
+        nc.vector.tensor_copy(
+            out=sg[:].rearrange("p (j q) -> p j q", j=4),
+            in_=sg_raw[:].rearrange("p (q j) -> p j q", j=4),
+        )
         turn_in(1, a_sb, a_ps)
         act_b(1)
         act_a(1)
@@ -445,23 +465,39 @@ def tile_prosody_predictor_backward_f3_kernel(
         turn_dz(0, 0)
         turn_dz(0, 1)
         stage1(2)
+        ga_view = ga_raw[:].rearrange("p g j -> p (g j)")
+        nc.vector.tensor_copy(out=ga[:], in_=ga_view)
+        nc.vector.tensor_scalar(out=nga[:], in0=ga_view, scalar1=-1.0, scalar2=None, op0=ALU.mult)
+        gb_view = gb_raw[:].rearrange("p g j -> p (g j)")
+        nc.vector.tensor_copy(out=gb[:], in_=gb_view)
+        nc.vector.tensor_scalar(out=ngb[:], in0=gb_view, scalar1=-1.0, scalar2=None, op0=ALU.mult)
         for part in range(2):
             for s in range(4 * part, 4 * part + 4):
                 affine(sn[0], sb[0], s, ngb, gb, True)
             for s in range(4 * part, 4 * part + 4):
                 affine(sq[0], sq[0], s, nga, ga, True)
-            factor_b_tanh(0, part, -1)
+        factor_b_tanh(0, 0, -1)
+        factor_b_tanh(0, 1, -1)
+        turn_in(2, b_sb, b_ps)
+        turn_in(2, a_sb, a_ps)
+        for k in DS:
+            dir_group(k, True)
         gate(0, 0)
         gate(0, 1)
         turn_dz(1, 0)
         turn_dz(1, 1)
-        dir_group(0)
-        dir_group(1)
-        dir_quant(0)
-        dir_group(2)
-        dir_quant(1)
-        turn_in(2, b_sb, b_ps)
-        turn_in(2, a_sb, a_ps)
+        norm_1(2, 0)
+        norm_1(2, 1)
+        if NG < 4:
+            factor_b_tanh_v(0, 0)
+            factor_b_tanh_v(0, 1)
+        dir_group(DV[0], False)
+        dir_group(DV[1], False)
+        dir_quant(DS[0])
+        dir_quant(DV[0])
+        dir_group(DV[2], False)
+        dir_quant(DV[1])
+        dir_quant(DV[2])
         act_b(2)
         act_a(2)
         turn_in(3, b_sb, b_ps)
@@ -477,11 +513,6 @@ def tile_prosody_predictor_backward_f3_kernel(
         turn_in(4, b_sb, b_ps)
         turn_in(4, a_sb, a_ps)
         dl_turn(3)
-        norm_1(2, 0)
-        norm_1(2, 1)
-        dir_group(3)
-        dir_quant(2)
-        dir_quant(3)
         for s in range(4):
             if s not in CV:
                 factor_a(1, s, False)
@@ -502,19 +533,18 @@ def tile_prosody_predictor_backward_f3_kernel(
             n2 = i + 2
             ys = i + 2
             gt = i + 1
-            if ok(i):
-                for which in range(2):
-                    for g in range(NH):
-                        branch(i, which, g)
+            branch(i, 0, 0)
+            branch(i, 0, 1)
             if ok(n2):
                 norm_2(n2)
-            if even and ok(i + 4):
-                dl_quant((i + 4) // 2)
-            if ok(i):
-                quant(i)
-
+            branch(i, 1, 0)
+            branch(i, 1, 1)
+            quant(i, 0)
             if ok(n2):
                 mean_1(n2)
+            if even and ok(i + 4):
+                dl_quant((i + 4) // 2)
+            quant(i, 1)
 
             if ok(i + 4):
                 act_b(i + 4)
@@ -523,6 +553,9 @@ def tile_prosody_predictor_backward_f3_kernel(
             if ok(i + 5):
                 turn_in(i + 5, b_sb, b_ps)
                 turn_in(i + 5, a_sb, a_ps)
+            if i == TILES - 1:
+                for repeat in range(3):
+                    stage1(i, False)
             if ok(i):
                 stage2(i)
             if even and ok(i + 6):

@@ -19,11 +19,10 @@ ACT = mybir.ActivationFunctionType
 
 P = 128
 TILES = ROWS // P
-NG = 4
-PLAIN = ()
+LASTC = 7
 DS = (0,)
 DV = (1, 2, 3)
-CV = (0, 1, 2, 3)
+CV = ((0, 0), (0, 1), (1, 0), (2, 0), (2, 1), (3, 0))
 HALF = 512
 NH = HID // HALF
 
@@ -58,7 +57,6 @@ def tile_prosody_predictor_backward_f3_kernel(
         ident = keep.tile([P, P], F32, name="ident")
         zero_col = keep.tile([P, 1], F32, name="zero_col")
         inv_raw = keep.tile([P, TILES], BF16, name="inv_raw")
-        inv = keep.tile([P, TILES], F32, name="inv")
         ga_raw = keep.tile([P, NH, 4], BF16, name="ga_raw")
         gb_raw = keep.tile([P, NH, 4], BF16, name="gb_raw")
         ga = keep.tile([P, 8], F32, name="ga")
@@ -66,7 +64,6 @@ def tile_prosody_predictor_backward_f3_kernel(
         gb = keep.tile([P, 8], F32, name="gb")
         ngb = keep.tile([P, 8], F32, name="ngb")
         sg_raw = keep.tile([P, HID], BF16, name="sg_raw")
-        sg = keep.tile([P, HID], BF16, name="sg")
         head_codes = keep.tile([P, HID], U32, name="head_codes", align_bytes=64)
         head_scales = keep.tile([P, HID], U8, name="head_scales", align_bytes=64)
         dir_codes = keep.tile([P, 4, ENC], U32, name="dir_codes", align_bytes=64)
@@ -113,12 +110,15 @@ def tile_prosody_predictor_backward_f3_kernel(
 
         head_grouped = {}
 
-        def head_group(g):
+        def head_group(g, shared):
             grouped = grps.tile([P, HALF, 4], BF16, name="grouped", align_bytes=64)
-            nc.vector.tensor_copy(
-                out=grouped[:].rearrange("p (j m) t -> p j m t", j=4),
-                in_=raw_sb["head", g][:].rearrange("p t (m j) -> p j m t", j=4),
-            )
+            dst = grouped[:].rearrange("p (j m) t -> p j m t", j=4)
+            src = raw_sb["head", g][:].rearrange("p t (m j) -> p j m t", j=4)
+            if shared:
+                nc.vector.tensor_copy(out=dst[:, :2], in_=src[:, :2])
+                nc.scalar.copy(out=dst[:, 2:], in_=src[:, 2:])
+            else:
+                nc.vector.tensor_copy(out=dst, in_=src)
             head_grouped[g] = grouped
 
         def head_quant(g, j):
@@ -176,9 +176,9 @@ def tile_prosody_predictor_backward_f3_kernel(
         def turn_in(i, src, ps):
             t = ps_in.tile([P, 512], F32, name="in_ps")
             words = src[i // 2][:].bitcast(F32)
-            for g in range(NH):
-                for u in range(2):
-                    s = 2 * g + u
+            for u in range(2):
+                for g in range(NH):
+                    s = 2 * u + g
                     nc.tensor.transpose(
                         t[:, s * P : (s + 1) * P],
                         words[:, i % 2, 256 * g + u : 256 * (g + 1) : 2],
@@ -186,38 +186,35 @@ def tile_prosody_predictor_backward_f3_kernel(
                     )
             ps[i] = t
 
-        def act(dst, i, ps, func, scale):
-            rows = slice(P * (i % 2), P * (i % 2 + 1))
+        def act(dst, i, ps, func):
             nc.scalar.activation(
-                out=dst[i // 2][:, :, rows].rearrange("p (s e) r -> p s e r", e=2),
-                in_=ps[i][:].bitcast(BF16).rearrange("p (s r e) -> p s e r", s=4, e=2),
+                out=dst[i // 2][:, :, i % 2, :].rearrange("p (u e) x -> p u e x", e=2),
+                in_=ps[i][:].bitcast(BF16).rearrange("p (u x e) -> p u e x", u=2, e=2),
                 func=func,
-                scale=scale,
             )
 
-        def act_a(i):
+        def act_ab(i):
             if i % 2 == 0:
-                th_t = two.tile([P, 8, 2 * P], F32, name="th")
-                sq_t = three.tile([P, 8, 2 * P], F32, name="sq")
-                th[i // 2], sq[i // 2] = th_t, sq_t
-            rows = slice(P * (i % 2), P * (i % 2 + 1))
-            act(th, i, a_ps, ACT.Tanh, 1.0)
+                for name, d in (("sb", sb), ("sn", sn), ("sq", sq)):
+                    t = three.tile([P, 4, 2, 2 * P], F32, name=name)
+                    d[i // 2] = t
+                th_t = two.tile([P, 4, 2, 2 * P], F32, name="th")
+                th[i // 2] = th_t
+            act(sb, i, b_ps, ACT.Sigmoid)
+            act(th, i, a_ps, ACT.Tanh)
+
+        def act_sq(i):
             nc.scalar.activation(
-                out=sq[i // 2][:, :, rows], in_=th[i // 2][:, :, rows], func=ACT.Square
+                out=sq[i // 2][:, :, i % 2, :], in_=th[i // 2][:, :, i % 2, :], func=ACT.Square
             )
 
-        def act_b(i):
-            if i % 2 == 0:
-                sb_t = three.tile([P, 8, 2 * P], F32, name="sb")
-                sn_t = three.tile([P, 8, 2 * P], F32, name="sn")
-                sb[i // 2], sn[i // 2] = sb_t, sn_t
-            act(sb, i, b_ps, ACT.Sigmoid, 1.0)
-
-        def affine(dst, src, s, minus, plus, on_vector):
+        def affine(dst, src, j, g, minus, plus, on_vector):
+            s = 4 * g + j
+            cols = slice(g * P, (g + 1) * P)
             if on_vector:
                 nc.vector.tensor_scalar(
-                    out=dst[:, s, :],
-                    in0=src[:, s, :],
+                    out=dst[:, j, :, cols],
+                    in0=src[:, j, :, cols],
                     scalar1=minus[:, s : s + 1],
                     scalar2=plus[:, s : s + 1],
                     op0=ALU.mult,
@@ -225,33 +222,39 @@ def tile_prosody_predictor_backward_f3_kernel(
                 )
             else:
                 nc.scalar.activation(
-                    out=dst[:, s, :],
-                    in_=src[:, s, :],
+                    out=dst[:, j, :, cols],
+                    in_=src[:, j, :, cols],
                     func=ACT.Identity,
                     scale=minus[:, s : s + 1],
                     bias=plus[:, s : s + 1],
                 )
 
-        def factor_a(pair, s, on_vector):
-            affine(sq[pair], sq[pair], s, nga, ga, on_vector)
+        def factor_a(pair, j, g, on_vector):
+            affine(sq[pair], sq[pair], j, g, nga, ga, on_vector)
 
-        def factor_b(pair, s, on_vector):
-            affine(sn[pair], sb[pair], s, ngb, gb, on_vector)
+        def factor_b(pair, j, g, on_vector):
+            affine(sn[pair], sb[pair], j, g, ngb, gb, on_vector)
 
-        def factor_b_tanh(pair, part, i):
-            if i >= 0:
-                tick = small.tile([P, 1], F32, name="tick")
-                nc.gpsimd.tensor_copy(out=tick[:], in_=sums[i][:, 3:4])
-            s = slice(4 * part, 4 * part + NG)
-            nc.gpsimd.tensor_tensor(
-                out=sn[pair][:, s, :], in0=th[pair][:, s, :], in1=sn[pair][:, s, :], op=ALU.mult
+        def scalar_factors_b(pair, part):
+            for j in (2 * part, 2 * part + 1):
+                for g in range(NH):
+                    factor_b(pair, j, g, False)
+
+        def scalar_factors_a(pair, part):
+            for j in (2 * part, 2 * part + 1):
+                for g in range(NH):
+                    if (j, g) not in CV or pair == LASTC:
+                        factor_a(pair, j, g, False)
+
+        def factor_b_tanh(pair, part, engine):
+            s = slice(2 * part, 2 * part + 2)
+            engine.tensor_tensor(
+                out=sn[pair][:, s], in0=th[pair][:, s], in1=sn[pair][:, s], op=ALU.mult
             )
 
-        def factor_b_tanh_v(pair, part):
-            s = slice(4 * part + NG, 4 * part + 4)
-            nc.vector.tensor_tensor(
-                out=sn[pair][:, s, :], in0=th[pair][:, s, :], in1=sn[pair][:, s, :], op=ALU.mult
-            )
+        def gpsimd_waits_for_means(i):
+            tick = small.tile([P, 1], F32, name="tick")
+            nc.gpsimd.tensor_copy(out=tick[:], in_=sums[i][:, 3:4])
 
         def stage1(i, fresh=True):
             cols = slice(P * (i % 2), P * (i % 2 + 1))
@@ -279,10 +282,10 @@ def tile_prosody_predictor_backward_f3_kernel(
                 dn[i], sums[i] = dn_t, s_t
             h = slice(g * HALF, (g + 1) * HALF)
             nc.vector.scalar_tensor_tensor(
-                out=dn[i][:, h],
-                in0=dh_ps[i, g][:],
-                scalar=inv[:, i : i + 1],
-                in1=sg[:, h],
+                out=dn[i][:, h].rearrange("p (j q) -> p j q", j=2),
+                in0=dh_ps[i, g][:].rearrange("p (j q) -> p j q", j=2),
+                scalar=inv_raw[:, i : i + 1],
+                in1=sg_raw[:].rearrange("p (q j) -> p j q", j=4)[:, 2 * g : 2 * g + 2, :],
                 op0=ALU.mult,
                 op1=ALU.mult,
                 accum_out=sums[i][:, g : g + 1],
@@ -320,41 +323,38 @@ def tile_prosody_predictor_backward_f3_kernel(
             )
             y[i] = t
 
-        def turn_dz(i, g):
+        def turn_dz(i, bank):
             t = ps_dz.tile([P, HALF], F32, name="dz_ps")
-            for j in range(4):
-                s = slice((j * NH + g) * P, (j * NH + g + 1) * P)
-                o = t[:, j * P : (j + 1) * P]
-                if j in PLAIN:
-                    nc.tensor.matmul(o, dn[i][:, s], ident[:], start=True, stop=False)
-                else:
-                    nc.tensor.matmul(o, dn[i][:, s], ident[:], start=True, stop=False, is_transpose=True)
+            for block in range(4):
+                s = slice(bank * HALF + block * P, bank * HALF + (block + 1) * P)
+                o = t[:, block * P : (block + 1) * P]
+                nc.tensor.matmul(o, dn[i][:, s], ident[:], start=True, stop=False, is_transpose=True)
                 nc.tensor.matmul(o, y[i][:, s], ident[:], start=False, stop=True, is_transpose=True)
-            dz_ps[i, g] = t
+            dz_ps[i, bank] = t
 
-        def gate(i, g):
-            if g == 0:
-                t = two.tile([P, 8, P], F32, name="q")
+        def gate(i, bank):
+            if bank == 0:
+                t = two.tile([P, 4, 2 * P], F32, name="q")
                 q[i] = t
-            rows = slice(P * (i % 2), P * (i % 2 + 1))
+            js = slice(2 * bank, 2 * bank + 2)
             nc.vector.tensor_tensor(
-                out=q[i][:, 4 * g : 4 * g + 4, :],
-                in0=dz_ps[i, g][:].rearrange("p (j r) -> p j r", j=4),
-                in1=sb[i // 2][:, 4 * g : 4 * g + 4, rows],
+                out=q[i][:, js, :],
+                in0=dz_ps[i, bank][:].rearrange("p (j x) -> p j x", j=2),
+                in1=sb[i // 2][:, js, i % 2, :],
                 op=ALU.mult,
             )
 
-        def branch(i, which, g):
-            if which == 0 and g == 0:
-                t = two.tile([P, 2 * NH * 4 * P], BF16, name="dab", align_bytes=64)
+        def branch(i, which):
+            if which == 0:
+                t = two.tile([P, 2 * HID], BF16, name="dab", align_bytes=64)
                 dab[i] = t
-            rows = slice(P * (i % 2), P * (i % 2 + 1))
             factor = (sq, sn)[which][i // 2]
-            at = (which * NH + g) * HALF
             nc.vector.tensor_tensor(
-                out=dab[i][:, at : at + HALF].rearrange("p (c i j) -> p c j i", i=4, j=4),
-                in0=q[i][:, 4 * g : 4 * g + 4, :].rearrange("p j (c i) -> p c j i", i=4),
-                in1=factor[:, 4 * g : 4 * g + 4, rows].rearrange("p j (c i) -> p c j i", i=4),
+                out=dab[i][:, which * HID : (which + 1) * HID].rearrange(
+                    "p (c i j) -> p c j i", i=4, j=4
+                ),
+                in0=q[i][:].rearrange("p j (c i) -> p c j i", i=4),
+                in1=factor[:, :, i % 2, :].rearrange("p j (c i) -> p c j i", i=4),
                 op=ALU.mult,
             )
 
@@ -408,9 +408,9 @@ def tile_prosody_predictor_backward_f3_kernel(
         warm = small.tile([P, 1], F32, name="warm")
         nc.scalar.activation(out=warm[:], in_=zero_col[:], func=ACT.Sigmoid)
 
+        load_raw(("head", 0), head_k[:, :, :HALF])
         load_dl(0)
-        for g in range(NH):
-            load_raw(("head", g), head_k[:, :, g * HALF : (g + 1) * HALF])
+        load_raw(("head", 1), head_k[:, :, HALF:])
         load_b(0)
         load_a(0)
         load_xn(0)
@@ -428,26 +428,21 @@ def tile_prosody_predictor_backward_f3_kernel(
 
         dl_turn(0)
         dl_copy(0)
-        head_group(0)
+        head_group(0, False)
         dl_quant(0)
+        head_group(1, True)
         turn_in(0, b_sb, b_ps)
         turn_in(0, a_sb, a_ps)
-        act_b(0)
-        act_a(0)
-        turn_in(1, b_sb, b_ps)
-        head_group(1)
+        act_ab(0)
+        act_sq(0)
         for j in range(4):
             for g in range(NH):
                 head_quant(g, j)
         stage1(0)
-        nc.vector.tensor_copy(out=inv[:], in_=inv_raw[:])
-        nc.vector.tensor_copy(
-            out=sg[:].rearrange("p (j q) -> p j q", j=4),
-            in_=sg_raw[:].rearrange("p (q j) -> p j q", j=4),
-        )
+        turn_in(1, b_sb, b_ps)
         turn_in(1, a_sb, a_ps)
-        act_b(1)
-        act_a(1)
+        act_ab(1)
+        act_sq(1)
         norm_1(0, 0)
         norm_1(0, 1)
         stage1(1)
@@ -455,9 +450,9 @@ def tile_prosody_predictor_backward_f3_kernel(
         norm_1(1, 0)
         norm_1(1, 1)
         mean_1(0)
-        correction(0)
         dl_turn(1)
         dl_copy(1)
+        correction(0)
         norm_2(1)
         dl_quant(1)
         mean_1(1)
@@ -471,13 +466,13 @@ def tile_prosody_predictor_backward_f3_kernel(
         gb_view = gb_raw[:].rearrange("p g j -> p (g j)")
         nc.vector.tensor_copy(out=gb[:], in_=gb_view)
         nc.vector.tensor_scalar(out=ngb[:], in0=gb_view, scalar1=-1.0, scalar2=None, op0=ALU.mult)
-        for part in range(2):
-            for s in range(4 * part, 4 * part + 4):
-                affine(sn[0], sb[0], s, ngb, gb, True)
-            for s in range(4 * part, 4 * part + 4):
-                affine(sq[0], sq[0], s, nga, ga, True)
-        factor_b_tanh(0, 0, -1)
-        factor_b_tanh(0, 1, -1)
+        for j in range(4):
+            for g in range(NH):
+                factor_b(0, j, g, True)
+        for j in range(4):
+            for g in range(NH):
+                factor_a(0, j, g, True)
+        factor_b_tanh(0, 0, nc.gpsimd)
         turn_in(2, b_sb, b_ps)
         turn_in(2, a_sb, a_ps)
         for k in DS:
@@ -488,9 +483,7 @@ def tile_prosody_predictor_backward_f3_kernel(
         turn_dz(1, 1)
         norm_1(2, 0)
         norm_1(2, 1)
-        if NG < 4:
-            factor_b_tanh_v(0, 0)
-            factor_b_tanh_v(0, 1)
+        factor_b_tanh(0, 1, nc.vector)
         dir_group(DV[0], False)
         dir_group(DV[1], False)
         dir_quant(DS[0])
@@ -498,12 +491,12 @@ def tile_prosody_predictor_backward_f3_kernel(
         dir_group(DV[2], False)
         dir_quant(DV[1])
         dir_quant(DV[2])
-        act_b(2)
-        act_a(2)
+        act_ab(2)
+        act_sq(2)
         turn_in(3, b_sb, b_ps)
         turn_in(3, a_sb, a_ps)
-        act_b(3)
-        act_a(3)
+        act_ab(3)
+        act_sq(3)
         dl_turn(2)
         dl_copy(2)
         load_dl(3)
@@ -513,10 +506,8 @@ def tile_prosody_predictor_backward_f3_kernel(
         turn_in(4, b_sb, b_ps)
         turn_in(4, a_sb, a_ps)
         dl_turn(3)
-        for s in range(4):
-            if s not in CV:
-                factor_a(1, s, False)
-            factor_b(1, s, False)
+        scalar_factors_b(1, 0)
+        scalar_factors_a(1, 0)
 
         def ok(i):
             return 0 <= i < TILES
@@ -533,12 +524,15 @@ def tile_prosody_predictor_backward_f3_kernel(
             n2 = i + 2
             ys = i + 2
             gt = i + 1
-            branch(i, 0, 0)
-            branch(i, 0, 1)
+            epair = (i + 2) // 2
+            branch(i, 0)
             if ok(n2):
                 norm_2(n2)
-            branch(i, 1, 0)
-            branch(i, 1, 1)
+            if epair < TILES // 2 and epair != LASTC:
+                for j, g in CV:
+                    if j // 2 == i % 2:
+                        factor_a(epair, j, g, True)
+            branch(i, 1)
             quant(i, 0)
             if ok(n2):
                 mean_1(n2)
@@ -547,7 +541,7 @@ def tile_prosody_predictor_backward_f3_kernel(
             quant(i, 1)
 
             if ok(i + 4):
-                act_b(i + 4)
+                act_ab(i + 4)
             if ok(i + 3):
                 stage1(i + 3)
             if ok(i + 5):
@@ -556,29 +550,24 @@ def tile_prosody_predictor_backward_f3_kernel(
             if i == TILES - 1:
                 for repeat in range(3):
                     stage1(i, False)
-            if ok(i):
-                stage2(i)
+            stage2(i)
             if even and ok(i + 6):
                 dl_copy((i + 6) // 2)
+            fpair = (i + 3) // 2
+            if fpair < TILES // 2:
+                scalar_factors_b(fpair, (i + 3) % 2)
             if ok(i + 4):
-                act_a(i + 4)
+                act_sq(i + 4)
             if not even and ok(i + 7):
                 dl_turn((i + 7) // 2)
-            fpair = (i + 3) // 2
-            part = (i + 3) % 2
-            if 0 <= fpair < TILES // 2:
-                for s in range(4 * part, 4 * part + 4):
-                    if s not in CV:
-                        factor_a(fpair, s, False)
-                    factor_b(fpair, s, False)
+            if fpair < TILES // 2:
+                scalar_factors_a(fpair, (i + 3) % 2)
             if ok(ys):
                 correction(ys)
-            if ok(i):
-                finish(i)
-            epair = (i + 2) // 2
-            if 0 <= epair < TILES // 2:
-                if NG:
-                    factor_b_tanh(epair, i % 2, i + 2 if 0 <= i < TILES - 2 else -1)
+            finish(i)
+            if epair < TILES // 2:
+                gpsimd_waits_for_means(i + 2)
+                factor_b_tanh(epair, i % 2, nc.gpsimd)
 
             if ok(gt):
                 gate(gt, 0)
@@ -589,9 +578,3 @@ def tile_prosody_predictor_backward_f3_kernel(
             if ok(ys):
                 turn_dz(ys, 0)
                 turn_dz(ys, 1)
-            if 0 <= epair < TILES // 2 and NG < 4:
-                factor_b_tanh_v(epair, i % 2)
-            if 0 <= epair < TILES // 2:
-                for s in range(4 * (i % 2), 4 * (i % 2) + 4):
-                    if s in CV:
-                        factor_a(epair, s, True)

from contextlib import ExitStack

import concourse.mybir as mybir
from concourse.masks import make_identity

ROWS, LOGITS, HID, ENC = 2048, 512, 1024, 512
UTTERANCES = 8

FLOPS = 2 * ROWS * LOGITS * HID + 2 * 2 * ROWS * HID * ENC

F32 = mybir.dt.float32
BF16 = mybir.dt.bfloat16
U32 = mybir.dt.uint32
U8 = mybir.dt.uint8
E4X4 = mybir.dt.float8_e4m3fn_x4
E5X4 = mybir.dt.float8_e5m2_x4
ALU = mybir.AluOpType
ACT = mybir.ActivationFunctionType

P = 128
TILES = ROWS // P
LASTC = 7
DS = (0,)
DV = (1, 2, 3)
CV = ((0, 0), (0, 1), (1, 0), (2, 0), (2, 1), (3, 0))
HALF = 512
NH = HID // HALF


def tile_prosody_predictor_backward_f3_kernel(
    tc, d_logits, head_w, spk_gain, normed, inv_std, pre_a, pre_b, gain_a, gain_b, dir_a, dir_b, out
):
    nc = tc.nc

    dl_rows = d_logits.rearrange("(p i) k -> p i k", i=TILES)
    xn_rows = normed.rearrange("(p i) h -> p i h", i=TILES)
    a_rows = pre_a.rearrange("(p i) h -> p i h", i=TILES)
    b_rows = pre_b.rearrange("(p i) h -> p i h", i=TILES)
    out_rows = out.rearrange("(p i) d -> p i d", i=TILES)
    head_k = head_w.rearrange("(p t) h -> p t h", t=4)
    dirs_k = [w.rearrange("(g p t) d -> g p t d", g=NH, t=4) for w in (dir_a, dir_b)]

    with ExitStack() as ctx:
        keep = ctx.enter_context(tc.tile_pool(name="keep", bufs=1))
        raws = ctx.enter_context(tc.tile_pool(name="raws", bufs=3))
        grps = ctx.enter_context(tc.tile_pool(name="grps", bufs=3))
        ins = ctx.enter_context(tc.tile_pool(name="ins", bufs=3))
        three = ctx.enter_context(tc.tile_pool(name="three", bufs=3))
        two = ctx.enter_context(tc.tile_pool(name="two", bufs=2))
        small = ctx.enter_context(tc.tile_pool(name="small", bufs=4))
        ps_dh = ctx.enter_context(tc.psum_pool(name="ps_dh", bufs=2))
        ps_dz = ctx.enter_context(tc.psum_pool(name="ps_dz", bufs=2))
        ps_in = ctx.enter_context(tc.psum_pool(name="ps_in", bufs=3))
        ps_out = ctx.enter_context(tc.psum_pool(name="ps_out", bufs=1))
        ctx.enter_context(tc.manual_schedule())

        ident = keep.tile([P, P], F32, name="ident")
        zero_col = keep.tile([P, 1], F32, name="zero_col")
        inv_raw = keep.tile([P, TILES], BF16, name="inv_raw")
        ga_raw = keep.tile([P, NH, 4], BF16, name="ga_raw")
        gb_raw = keep.tile([P, NH, 4], BF16, name="gb_raw")
        ga = keep.tile([P, 8], F32, name="ga")
        nga = keep.tile([P, 8], F32, name="nga")
        gb = keep.tile([P, 8], F32, name="gb")
        ngb = keep.tile([P, 8], F32, name="ngb")
        sg_raw = keep.tile([P, HID], BF16, name="sg_raw")
        head_codes = keep.tile([P, HID], U32, name="head_codes", align_bytes=64)
        head_scales = keep.tile([P, HID], U8, name="head_scales", align_bytes=64)
        dir_codes = keep.tile([P, 4, ENC], U32, name="dir_codes", align_bytes=64)
        dir_scales = keep.tile([P, 4, ENC], U8, name="dir_scales", align_bytes=64)

        junk = keep.tile([P, HID], F32, name="junk")

        dl_sb, a_sb, b_sb, xn_sb = {}, {}, {}, {}
        raw_sb = {}
        dl_ps, dl_grp, dl_codes, dl_scales = {}, {}, {}, {}
        a_ps, b_ps, dh_ps, dz_ps, out_ps = {}, {}, {}, {}, {}
        th, sb, sn, sq = {}, {}, {}, {}
        dn, y, q, sums = {}, {}, {}, {}
        dab, codes, scales, out_sb = {}, {}, {}, {}

        def load_dl(pair):
            t = ins.tile([P, 2, LOGITS], BF16, name="dl_sb")
            nc.sync.dma_start(out=t[:], in_=dl_rows[:, 2 * pair : 2 * pair + 2, :])
            dl_sb[pair] = t

        def load_ab(pair):
            load_b(pair)
            load_a(pair)

        def load_a(pair):
            ta = ins.tile([P, 2, HID], BF16, name="a_sb")
            nc.sync.dma_start(out=ta[:], in_=a_rows[:, 2 * pair : 2 * pair + 2, :])
            a_sb[pair] = ta

        def load_b(pair):
            tb = ins.tile([P, 2, HID], BF16, name="b_sb")
            nc.sync.dma_start(out=tb[:], in_=b_rows[:, 2 * pair : 2 * pair + 2, :])
            b_sb[pair] = tb

        def load_xn(pair):
            t = ins.tile([P, 2, HID], BF16, name="xn_sb")
            nc.sync.dma_start(out=t[:], in_=xn_rows[:, 2 * pair : 2 * pair + 2, :])
            xn_sb[pair] = t

        def load_raw(key, view):
            t = raws.tile([P, 4, HALF], BF16, name="raw_sb")
            nc.sync.dma_start(out=t[:], in_=view)
            raw_sb[key] = t

        head_grouped = {}

        def head_group(g, shared):
            grouped = grps.tile([P, HALF, 4], BF16, name="grouped", align_bytes=64)
            dst = grouped[:].rearrange("p (j m) t -> p j m t", j=4)
            src = raw_sb["head", g][:].rearrange("p t (m j) -> p j m t", j=4)
            if shared:
                nc.vector.tensor_copy(out=dst[:, :2], in_=src[:, :2])
                nc.scalar.copy(out=dst[:, 2:], in_=src[:, 2:])
            else:
                nc.vector.tensor_copy(out=dst, in_=src)
            head_grouped[g] = grouped

        def head_quant(g, j):
            at = (j * NH + g) * P
            nc.vector.quantize_mx(
                out=head_codes[:, at : at + P].bitcast(E4X4),
                scales=head_scales[:, at : at + P],
                in_=head_grouped[g][:, j * P : (j + 1) * P, :].rearrange("p c t -> p (c t)"),
            )

        dir_grouped = {}

        def dir_group(k, on_scalar):
            grouped = grps.tile([P, HALF, 4], BF16, name="grouped", align_bytes=64)
            dst = grouped[:].rearrange("p (c i) t -> p c t i", i=4)
            src = raw_sb["dir", k][:].rearrange("p t (c i) -> p c t i", i=4)
            if on_scalar:
                nc.scalar.copy(out=dst, in_=src)
            else:
                nc.vector.tensor_copy(out=dst, in_=src)
            dir_grouped[k] = grouped

        def dir_quant(k):
            nc.vector.quantize_mx(
                out=dir_codes[:, k, :].bitcast(E4X4),
                scales=dir_scales[:, k, :],
                in_=dir_grouped[k][:].rearrange("p c t -> p (c t)"),
            )

        def dl_turn(pair):
            t = ps_in.tile([P, 512], F32, name="in_ps")
            words = dl_sb[pair][:].bitcast(F32)
            for r in range(2):
                for u in range(2):
                    s = 2 * r + u
                    nc.tensor.transpose(
                        t[:, s * P : (s + 1) * P], words[:, r, u : LOGITS // 2 : 2], ident[:]
                    )
            dl_ps[pair] = t

        def dl_copy(pair):
            grouped = two.tile([P, 2 * P * 4], BF16, name="dl_grp", align_bytes=64)
            nc.scalar.copy(
                out=grouped[:].bitcast(F32).rearrange("p (i r u) -> p i r u", i=2, u=2),
                in_=dl_ps[pair][:].rearrange("p (i u r) -> p i r u", i=2, u=2),
            )
            dl_grp[pair] = grouped

        def dl_quant(pair):
            c = three.tile([P, 2 * P], U32, name="dl_codes", align_bytes=64)
            s = three.tile([P, 2 * P], U8, name="dl_scales", align_bytes=64)
            nc.vector.quantize_mx(out=c[:].bitcast(E4X4), scales=s[:], in_=dl_grp[pair][:])
            dl_codes[pair], dl_scales[pair] = c, s

        def turn_in(i, src, ps):
            t = ps_in.tile([P, 512], F32, name="in_ps")
            words = src[i // 2][:].bitcast(F32)
            for u in range(2):
                for g in range(NH):
                    s = 2 * u + g
                    nc.tensor.transpose(
                        t[:, s * P : (s + 1) * P],
                        words[:, i % 2, 256 * g + u : 256 * (g + 1) : 2],
                        ident[:],
                    )
            ps[i] = t

        def act(dst, i, ps, func):
            nc.scalar.activation(
                out=dst[i // 2][:, :, i % 2, :].rearrange("p (u e) x -> p u e x", e=2),
                in_=ps[i][:].bitcast(BF16).rearrange("p (u x e) -> p u e x", u=2, e=2),
                func=func,
            )

        def act_ab(i):
            if i % 2 == 0:
                for name, d in (("sb", sb), ("sn", sn), ("sq", sq)):
                    t = three.tile([P, 4, 2, 2 * P], F32, name=name)
                    d[i // 2] = t
                th_t = two.tile([P, 4, 2, 2 * P], F32, name="th")
                th[i // 2] = th_t
            act(sb, i, b_ps, ACT.Sigmoid)
            act(th, i, a_ps, ACT.Tanh)

        def act_sq(i):
            nc.scalar.activation(
                out=sq[i // 2][:, :, i % 2, :], in_=th[i // 2][:, :, i % 2, :], func=ACT.Square
            )

        def affine(dst, src, j, g, minus, plus, on_vector):
            s = 4 * g + j
            cols = slice(g * P, (g + 1) * P)
            if on_vector:
                nc.vector.tensor_scalar(
                    out=dst[:, j, :, cols],
                    in0=src[:, j, :, cols],
                    scalar1=minus[:, s : s + 1],
                    scalar2=plus[:, s : s + 1],
                    op0=ALU.mult,
                    op1=ALU.add,
                )
            else:
                nc.scalar.activation(
                    out=dst[:, j, :, cols],
                    in_=src[:, j, :, cols],
                    func=ACT.Identity,
                    scale=minus[:, s : s + 1],
                    bias=plus[:, s : s + 1],
                )

        def factor_a(pair, j, g, on_vector):
            affine(sq[pair], sq[pair], j, g, nga, ga, on_vector)

        def factor_b(pair, j, g, on_vector):
            affine(sn[pair], sb[pair], j, g, ngb, gb, on_vector)

        def scalar_factors_b(pair, part):
            for j in (2 * part, 2 * part + 1):
                for g in range(NH):
                    factor_b(pair, j, g, False)

        def scalar_factors_a(pair, part):
            for j in (2 * part, 2 * part + 1):
                for g in range(NH):
                    if (j, g) not in CV or pair == LASTC:
                        factor_a(pair, j, g, False)

        def factor_b_tanh(pair, part, engine):
            s = slice(2 * part, 2 * part + 2)
            engine.tensor_tensor(
                out=sn[pair][:, s], in0=th[pair][:, s], in1=sn[pair][:, s], op=ALU.mult
            )

        def gpsimd_waits_for_means(i):
            tick = small.tile([P, 1], F32, name="tick")
            nc.gpsimd.tensor_copy(out=tick[:], in_=sums[i][:, 3:4])

        def stage1(i, fresh=True):
            cols = slice(P * (i % 2), P * (i % 2 + 1))
            for g in range(NH):
                if fresh:
                    t = ps_dh.tile([P, HALF], F32, name="dh_ps")
                else:
                    t = dh_ps[i, g]
                h = slice(g * HALF, (g + 1) * HALF)
                nc.tensor.matmul_mx(
                    out=t[:],
                    lhsT=dl_codes[i // 2][:, cols].bitcast(E4X4),
                    lhsT_scale=dl_scales[i // 2][:, cols],
                    rhs=head_codes[:, h].bitcast(E4X4),
                    rhs_scale=head_scales[:, h],
                    start=True,
                    stop=True,
                )
                dh_ps[i, g] = t

        def norm_1(i, g):
            if g == 0:
                dn_t = three.tile([P, HID], F32, name="dn")
                s_t = small.tile([P, 4], F32, name="sums")
                dn[i], sums[i] = dn_t, s_t
            h = slice(g * HALF, (g + 1) * HALF)
            nc.vector.scalar_tensor_tensor(
                out=dn[i][:, h].rearrange("p (j q) -> p j q", j=2),
                in0=dh_ps[i, g][:].rearrange("p (j q) -> p j q", j=2),
                scalar=inv_raw[:, i : i + 1],
                in1=sg_raw[:].rearrange("p (q j) -> p j q", j=4)[:, 2 * g : 2 * g + 2, :],
                op0=ALU.mult,
                op1=ALU.mult,
                accum_out=sums[i][:, g : g + 1],
            )

        def norm_2(i):
            nc.vector.scalar_tensor_tensor(
                out=junk[:].rearrange("p (j q) -> p j q", j=4),
                in0=dn[i][:].rearrange("p (j q) -> p j q", j=4),
                scalar=-1.0 / HID,
                in1=xn_sb[i // 2][:, i % 2, :].rearrange("p (q j) -> p j q", j=4),
                op0=ALU.mult,
                op1=ALU.mult,
                accum_out=sums[i][:, 2:3],
            )

        def mean_1(i):
            nc.vector.tensor_scalar(
                out=sums[i][:, 3:4],
                in0=sums[i][:, 0:1],
                scalar1=sums[i][:, 1:2],
                scalar2=-1.0 / HID,
                op0=ALU.add,
                op1=ALU.mult,
            )

        def correction(i):
            t = two.tile([P, HID], F32, name="y")
            nc.scalar.activation(
                out=t[:].rearrange("p (j q) -> p j q", j=4),
                in_=xn_sb[i // 2][:, i % 2, :].rearrange("p (q j) -> p j q", j=4),
                func=ACT.Identity,
                scale=sums[i][:, 2:3],
                bias=sums[i][:, 3:4],
            )
            y[i] = t

        def turn_dz(i, bank):
            t = ps_dz.tile([P, HALF], F32, name="dz_ps")
            for block in range(4):
                s = slice(bank * HALF + block * P, bank * HALF + (block + 1) * P)
                o = t[:, block * P : (block + 1) * P]
                nc.tensor.matmul(o, dn[i][:, s], ident[:], start=True, stop=False, is_transpose=True)
                nc.tensor.matmul(o, y[i][:, s], ident[:], start=False, stop=True, is_transpose=True)
            dz_ps[i, bank] = t

        def gate(i, bank):
            if bank == 0:
                t = two.tile([P, 4, 2 * P], F32, name="q")
                q[i] = t
            js = slice(2 * bank, 2 * bank + 2)
            nc.vector.tensor_tensor(
                out=q[i][:, js, :],
                in0=dz_ps[i, bank][:].rearrange("p (j x) -> p j x", j=2),
                in1=sb[i // 2][:, js, i % 2, :],
                op=ALU.mult,
            )

        def branch(i, which):
            if which == 0:
                t = two.tile([P, 2 * HID], BF16, name="dab", align_bytes=64)
                dab[i] = t
            factor = (sq, sn)[which][i // 2]
            nc.vector.tensor_tensor(
                out=dab[i][:, which * HID : (which + 1) * HID].rearrange(
                    "p (c i j) -> p c j i", i=4, j=4
                ),
                in0=q[i][:].rearrange("p j (c i) -> p c j i", i=4),
                in1=factor[:, :, i % 2, :].rearrange("p j (c i) -> p c j i", i=4),
                op=ALU.mult,
            )

        def quant(i, which):
            if which == 0:
                c = two.tile([P, 4 * P], U32, name="codes", align_bytes=64)
                s = two.tile([P, 4 * P], U8, name="scales", align_bytes=64)
                codes[i], scales[i] = c, s
            half = slice(which * 2 * P, (which + 1) * 2 * P)
            nc.vector.quantize_mx(
                out=codes[i][:, half].bitcast(E5X4),
                scales=scales[i][:, half],
                in_=dab[i][:, which * HID : (which + 1) * HID],
            )

        def stage2(i):
            t = ps_out.tile([P, ENC], F32, name="out_ps")
            for k in range(4):
                cols = slice(k * P, (k + 1) * P)
                nc.tensor.matmul_mx(
                    out=t[:],
                    lhsT=codes[i][:, cols].bitcast(E5X4),
                    lhsT_scale=scales[i][:, cols],
                    rhs=dir_codes[:, k, :].bitcast(E4X4),
                    rhs_scale=dir_scales[:, k, :],
                    start=(k == 0),
                    stop=(k == 3),
                )
            out_ps[i] = t

        def finish(i):
            t = three.tile([P, ENC], F32, name="out_sb")
            if i < TILES - 1:
                nc.scalar.copy(out=t[:], in_=out_ps[i][:])
                nc.sync.dma_start(out=out_rows[:, i, :], in_=t[:])
            else:
                half = ENC // 2
                t2 = keep.tile([P, half], F32, name="out_sb2")
                nc.scalar.copy(out=t[:, :half], in_=out_ps[i][:, :half])
                nc.sync.dma_start(out=out_rows[:, i, :half], in_=t[:, :half])
                nc.scalar.copy(out=t2[:], in_=out_ps[i][:, half:])
                nc.scalar.dma_start(out=out_rows[:, i, half:], in_=t2[:])

        nc.vector.memset(zero_col[:], 0.0)
        make_identity(nc, ident[:])
        nc.scalar.dma_start(out=inv_raw[:], in_=inv_std.rearrange("(p i) -> p i", i=TILES))
        for u in range(UTTERANCES):
            nc.scalar.dma_start(
                out=sg_raw[16 * u : 16 * (u + 1), :], in_=spk_gain[u, :].partition_broadcast(16)
            )
        warm = small.tile([P, 1], F32, name="warm")
        nc.scalar.activation(out=warm[:], in_=zero_col[:], func=ACT.Sigmoid)

        load_raw(("head", 0), head_k[:, :, :HALF])
        load_dl(0)
        load_raw(("head", 1), head_k[:, :, HALF:])
        load_b(0)
        load_a(0)
        load_xn(0)
        nc.sync.dma_start(out=ga_raw[:], in_=gain_a.rearrange("(g p j) -> p g j", g=NH, j=4))
        nc.sync.dma_start(out=gb_raw[:], in_=gain_b.rearrange("(g p j) -> p g j", g=NH, j=4))
        load_dl(1)
        for k in DS + DV:
            load_raw(("dir", k), dirs_k[k // NH][k % NH])
        load_b(1)
        load_a(1)
        load_xn(1)
        load_dl(2)
        load_ab(2)
        load_xn(2)

        dl_turn(0)
        dl_copy(0)
        head_group(0, False)
        dl_quant(0)
        head_group(1, True)
        turn_in(0, b_sb, b_ps)
        turn_in(0, a_sb, a_ps)
        act_ab(0)
        act_sq(0)
        for j in range(4):
            for g in range(NH):
                head_quant(g, j)
        stage1(0)
        turn_in(1, b_sb, b_ps)
        turn_in(1, a_sb, a_ps)
        act_ab(1)
        act_sq(1)
        norm_1(0, 0)
        norm_1(0, 1)
        stage1(1)
        norm_2(0)
        norm_1(1, 0)
        norm_1(1, 1)
        mean_1(0)
        dl_turn(1)
        dl_copy(1)
        correction(0)
        norm_2(1)
        dl_quant(1)
        mean_1(1)
        correction(1)
        turn_dz(0, 0)
        turn_dz(0, 1)
        stage1(2)
        ga_view = ga_raw[:].rearrange("p g j -> p (g j)")
        nc.vector.tensor_copy(out=ga[:], in_=ga_view)
        nc.vector.tensor_scalar(out=nga[:], in0=ga_view, scalar1=-1.0, scalar2=None, op0=ALU.mult)
        gb_view = gb_raw[:].rearrange("p g j -> p (g j)")
        nc.vector.tensor_copy(out=gb[:], in_=gb_view)
        nc.vector.tensor_scalar(out=ngb[:], in0=gb_view, scalar1=-1.0, scalar2=None, op0=ALU.mult)
        for j in range(4):
            for g in range(NH):
                factor_b(0, j, g, True)
        for j in range(4):
            for g in range(NH):
                factor_a(0, j, g, True)
        factor_b_tanh(0, 0, nc.gpsimd)
        turn_in(2, b_sb, b_ps)
        turn_in(2, a_sb, a_ps)
        for k in DS:
            dir_group(k, True)
        gate(0, 0)
        gate(0, 1)
        turn_dz(1, 0)
        turn_dz(1, 1)
        norm_1(2, 0)
        norm_1(2, 1)
        factor_b_tanh(0, 1, nc.vector)
        dir_group(DV[0], False)
        dir_group(DV[1], False)
        dir_quant(DS[0])
        dir_quant(DV[0])
        dir_group(DV[2], False)
        dir_quant(DV[1])
        dir_quant(DV[2])
        act_ab(2)
        act_sq(2)
        turn_in(3, b_sb, b_ps)
        turn_in(3, a_sb, a_ps)
        act_ab(3)
        act_sq(3)
        dl_turn(2)
        dl_copy(2)
        load_dl(3)
        load_ab(3)
        load_dl(4)
        load_ab(4)
        turn_in(4, b_sb, b_ps)
        turn_in(4, a_sb, a_ps)
        dl_turn(3)
        scalar_factors_b(1, 0)
        scalar_factors_a(1, 0)

        def ok(i):
            return 0 <= i < TILES

        for i in range(TILES):
            even = i % 2 == 0
            if not even and (i + 9) // 2 < TILES // 2:
                load_dl((i + 9) // 2)
                load_ab((i + 9) // 2)
            if even and (i + 6) // 2 < TILES // 2:
                load_xn((i + 6) // 2)

            n1 = i + 3
            n2 = i + 2
            ys = i + 2
            gt = i + 1
            epair = (i + 2) // 2
            branch(i, 0)
            if ok(n2):
                norm_2(n2)
            if epair < TILES // 2 and epair != LASTC:
                for j, g in CV:
                    if j // 2 == i % 2:
                        factor_a(epair, j, g, True)
            branch(i, 1)
            quant(i, 0)
            if ok(n2):
                mean_1(n2)
            if even and ok(i + 4):
                dl_quant((i + 4) // 2)
            quant(i, 1)

            if ok(i + 4):
                act_ab(i + 4)
            if ok(i + 3):
                stage1(i + 3)
            if ok(i + 5):
                turn_in(i + 5, b_sb, b_ps)
                turn_in(i + 5, a_sb, a_ps)
            if i == TILES - 1:
                for repeat in range(3):
                    stage1(i, False)
            stage2(i)
            if even and ok(i + 6):
                dl_copy((i + 6) // 2)
            fpair = (i + 3) // 2
            if fpair < TILES // 2:
                scalar_factors_b(fpair, (i + 3) % 2)
            if ok(i + 4):
                act_sq(i + 4)
            if not even and ok(i + 7):
                dl_turn((i + 7) // 2)
            if fpair < TILES // 2:
                scalar_factors_a(fpair, (i + 3) % 2)
            if ok(ys):
                correction(ys)
            finish(i)
            if epair < TILES // 2:
                gpsimd_waits_for_means(i + 2)
                factor_b_tanh(epair, i % 2, nc.gpsimd)

            if ok(gt):
                gate(gt, 0)
                gate(gt, 1)
            if ok(n1):
                norm_1(n1, 0)
                norm_1(n1, 1)
            if ok(ys):
                turn_dz(ys, 0)
                turn_dz(ys, 1)
